import numpy as np
import ml_dtypes


def mxq(x, axis, fmt="e4m3"):
    dtype, down = {"e4m3": (ml_dtypes.float8_e4m3fn, 7), "e5m2": (ml_dtypes.float8_e5m2, 14)}[fmt]
    v = np.moveaxis(np.asarray(x, np.float32).astype(ml_dtypes.bfloat16).astype(np.float64), axis, -1)
    blocks = v.reshape(v.shape[:-1] + (-1, 32))
    amax = np.abs(blocks).max(-1, keepdims=True)
    byte = np.maximum(np.where(amax > 0, np.frexp(amax)[1] - 1 + 127, 0) - down, 1)
    scale = np.exp2(byte - 127.0)
    codes = (blocks / scale).astype(np.float32).astype(dtype).astype(np.float64)
    return np.moveaxis((codes * scale).reshape(v.shape), -1, axis)


WIDE = False


def mx_kscale(k):
    if not WIDE:
        return np.ones(k)
    levels = np.array([10, -10, 5, -5, 0])
    if k % 512:
        return np.exp2(np.random.permutation(np.resize(levels, k // 32))).repeat(32)
    a = np.empty((k // 512, 16))
    for p in range(k // 512):
        a[p, :8] = np.random.permutation(np.resize(levels, 8))
        for g in range(8):
            far = levels[np.abs(levels - a[p, g]) >= 10]
            a[p, g + 8] = far[np.random.randint(len(far))]
    return np.exp2(a.ravel()).repeat(32)


def f64(x):
    return np.asarray(x).astype(np.float64)


E2M1 = np.array([0.0, 0.5, 1.0, 1.5, 2.0, 3.0, 4.0, 6.0, -0.0, -0.5, -1.0, -1.5, -2.0, -3.0, -4.0, -6.0])


def pack_weight(w, fmt):
    k, n = w.shape
    w = f64(np.asarray(w, np.float32).astype(ml_dtypes.bfloat16)).reshape(k // 32, 32, n)
    amax = np.abs(w).max(1)
    if fmt == "e4m3":
        byte = np.frexp(amax)[1] - 1 + 127 - 7
    else:
        mant, ex = np.frexp(amax / 6.0)
        byte = np.where(mant > 0.5, ex, ex - 1) + 127
    byte = np.clip(np.where(amax > 0, byte, 1), 1, 254)
    scaled = (w * np.exp2(127.0 - byte)[:, None, :]).reshape(k, n).astype(np.float32)
    by_word = np.ascontiguousarray(scaled.reshape(k // 512, 128, 4, n).transpose(0, 1, 3, 2))
    if fmt == "e4m3":
        words = by_word.astype(ml_dtypes.float8_e4m3fn).view(np.uint8)
    else:
        c = by_word.astype(ml_dtypes.float4_e2m1fn).view(np.uint8) & 0xF
        words = (c[..., 0::2] | (c[..., 1::2] << 4)).reshape(k // 512, 128, 2 * n)
    return np.ascontiguousarray(words), np.ascontiguousarray(byte.astype(np.uint8).reshape(k // 512, 16, n))


def unpack_weight(words, scales, fmt):
    g, _, n = scales.shape
    words = np.ascontiguousarray(words).reshape(g, 128, n, -1)
    if fmt == "e4m3":
        vals = words.view(ml_dtypes.float8_e4m3fn).astype(np.float64)
    else:
        nib = np.empty((g, 128, n, 4), np.uint8)
        nib[..., 0::2] = words & 0xF
        nib[..., 1::2] = words >> 4
        vals = E2M1[nib]
    vals = vals * np.repeat(np.exp2(scales.astype(np.float64) - 127.0), 8, axis=1)[..., None]
    return vals.transpose(0, 1, 3, 2).reshape(g * 512, n)


def silu(v):
    return v / (1.0 + np.exp(-np.maximum(v, -700.0)))


K, M, T = 2048, 512, 1024


def setup_inputs():
    n = np.random.standard_normal
    s = mx_kscale(K)[:, None]
    p_w4 = pack_weight(n((K, M)) / np.sqrt(K) / s, "e2m1")
    p_w8 = pack_weight(n((K, M)) / np.sqrt(K) / s, "e4m3")
    return {
        "x": (n((K, T)) * s).astype(np.float32),
        "w4_words": p_w4[0],
        "w4_scales": p_w4[1],
        "w8_words": p_w8[0],
        "w8_scales": p_w8[1],
    }


def reference(x, w4_words, w4_scales, w8_words, w8_scales):
    x_ = mxq(f64(x), 0, "e4m3")
    w4_ = unpack_weight(w4_words, w4_scales, "e2m1")
    w8_ = unpack_weight(w8_words, w8_scales, "e4m3")
    y = w4_.T @ x_
    u = w8_.T @ x_
    y = silu(y) * u
    return y

@@ -1,0 +1,272 @@
+from contextlib import ExitStack
+
+import concourse.mybir as mybir
+
+K, M, T = 2048, 512, 1024
+FLOPS = 2 * 2 * K * M * T
+
+F32 = mybir.dt.float32
+BF16 = mybir.dt.bfloat16
+I32 = mybir.dt.int32
+U32 = mybir.dt.uint32
+U8 = mybir.dt.uint8
+FP8X4 = mybir.dt.float8_e4m3fn_x4
+FP4X4 = mybir.dt.float4_e2m1fn_x4
+ACT = mybir.ActivationFunctionType
+ALU = mybir.AluOpType
+
+P = 128
+PASSES = K // 512
+HALF = 512
+M_TILES = M // 128
+V_COLS = 320
+
+
+def tile_mix_glu48_fm_none_kernel(tc, x, w4_words, w4_scales, w8_words, w8_scales, out):
+    nc = tc.nc
+    with ExitStack() as ctx:
+        keep = ctx.enter_context(tc.tile_pool(name="keep", bufs=1))
+        psum = ctx.enter_context(tc.psum_pool(name="psum", bufs=1))
+        ctx.enter_context(tc.manual_schedule())
+
+        sc4 = keep.tile([P, PASSES * M], U8, align_bytes=64, name="sc4")
+        sc8 = keep.tile([P, M], U8, align_bytes=64, name="sc8")
+        dummy = keep.tile([P, 8], F32, align_bytes=64, name="dummy")
+        nc.vector.memset(sc8[:].bitcast(I32), 0)
+        nc.vector.memset(sc4[:].bitcast(I32), 0)
+        nc.vector.memset(dummy[:], 0.0)
+
+        raw = {}
+        w4 = {}
+        w8 = {}
+
+        def load_x(h, a, pieces=1, which=(0, 1)):
+            width = HALF // pieces
+            for c in which[:pieces]:
+                t = keep.tile([P, 4, width], F32, align_bytes=64, name="raw_%d_%d_%d" % (h, a, c))
+                for lo in range(0, width, 256):
+                    raw[h, a, width * c + lo] = t[:, :, lo : lo + 256]
+                nc.sync.dma_start(
+                    out=t[:],
+                    in_=x[512 * a : 512 * (a + 1), HALF * h + width * c : HALF * h + width * (c + 1)].rearrange(
+                        "(p j) w -> p j w", j=4
+                    ),
+                )
+
+        def load_w8(a):
+            w8[a] = keep.tile([P, 4 * M], U8, align_bytes=64, name="w8_%d" % a)
+            nc.sync.dma_start(out=w8[a][:].bitcast(I32), in_=w8_words[a].rearrange("p n i -> p (n i)").bitcast(I32))
+
+        def load_w4(a, n):
+            t = keep.tile([P, n, 2 * M], U8, align_bytes=64, name="w4_%d" % a)
+            for i in range(n):
+                w4[a + i] = t[:, i, :]
+            nc.sync.dma_start(
+                out=t[:].bitcast(I32), in_=w4_words[a : a + n].rearrange("a p b -> p a b").bitcast(I32)
+            )
+
+        def load_sc8():
+            for q in range(4):
+                nc.scalar.dma_start(
+                    out=sc8[32 * q : 32 * q + 16, :].bitcast(I32),
+                    in_=w8_scales[:, 4 * q : 4 * q + 4, :].bitcast(I32),
+                )
+
+        def load_sc4():
+            for q in range(4):
+                nc.scalar.dma_start(
+                    out=sc4[32 * q : 32 * q + 4, :].bitcast(I32).rearrange("r (a n) -> r a n", a=PASSES),
+                    in_=w4_scales[:, 4 * q : 4 * q + 4, :].bitcast(I32).rearrange("a r n -> r a n"),
+                )
+
+        load_sc8()
+        nc.scalar.activation(out=dummy[:, 0:1], in_=dummy[:, 1:2], func=ACT.Silu)
+        load_x(0, 0, 2)
+        load_w4(0, 1)
+        load_w8(0)
+        load_x(0, 1)
+        load_sc4()
+        load_w4(1, 3)
+        load_w8(1)
+        load_x(0, 2)
+        load_x(0, 3)
+        load_w8(2)
+        load_x(1, 0, 2)
+        load_w8(3)
+        for a in range(1, PASSES):
+            load_x(1, a, 2)
+
+        grouped = {}
+        codes = {}
+        scales = {}
+
+        def interleave(engine_copy, h, a, lo, hi):
+            base = lo // 256 * 256
+            engine_copy(
+                out=grouped[h, a][:, lo:hi, :].rearrange("p (c i) t -> p c t i", i=4),
+                in_=raw[h, a, base][:, :, lo - base : hi - base].rearrange("p t (c i) -> p c t i", i=4),
+            )
+
+        def tiles(h, a):
+            grouped[h, a] = keep.tile([P, HALF, 4], BF16, align_bytes=64, name="grouped_%d_%d" % (h, a))
+            codes[h, a] = keep.tile([P, HALF], U32, align_bytes=64, name="codes_%d_%d" % (h, a))
+            scales[h, a] = keep.tile([P, HALF], U8, align_bytes=64, name="scales_%d_%d" % (h, a))
+
+        def quantize(h, a, lo):
+            nc.vector.quantize_mx(
+                out=codes[h, a][:, lo : lo + 256].bitcast(FP8X4),
+                scales=scales[h, a][:, lo : lo + 256],
+                in_=grouped[h, a][:, lo : lo + 256, :].rearrange("p w t -> p (w t)"),
+            )
+
+        def copies_whole(h, a):
+            tiles(h, a)
+            interleave(nc.vector.tensor_copy, h, a, 0, 256)
+            interleave(nc.vector.tensor_copy, h, a, 256, V_COLS)
+            interleave(nc.scalar.copy, h, a, V_COLS, HALF)
+
+        def copy_piece_v(h, a, lo):
+            interleave(nc.vector.tensor_copy, h, a, lo, lo + V_COLS // 2)
+
+        def copy_piece_s(h, a, lo):
+            interleave(nc.scalar.copy, h, a, lo + V_COLS // 2, lo + 256)
+
+        def prepare_pieces(h, a):
+            tiles(h, a)
+            for lo in (0, 256):
+                copy_piece_v(h, a, lo)
+                copy_piece_s(h, a, lo)
+                quantize(h, a, lo)
+
+        g = {}
+        u = {}
+
+        def pass_g(h, a, m, lo, hi):
+            nc.tensor.matmul_mx(
+                out=g[h, m][:, lo:hi],
+                lhsT=w4[a][:, 256 * m : 256 * (m + 1)].bitcast(FP4X4),
+                lhsT_scale=sc4[:, M * a + 128 * m : M * a + 128 * (m + 1)],
+                rhs=codes[h, a][:, lo:hi].bitcast(FP8X4),
+                rhs_scale=scales[h, a][:, lo:hi],
+                start=(a == 0),
+                stop=(a == PASSES - 1 and hi == HALF),
+            )
+
+        def pass_u(h, a, m, lo, hi):
+            nc.tensor.matmul_mx(
+                out=u[h, m][:, lo:hi],
+                lhsT=w8[a][:, 512 * m : 512 * (m + 1)].bitcast(FP8X4),
+                lhsT_scale=sc8[4 * a : P, 128 * m : 128 * (m + 1)],
+                rhs=codes[h, a][:, lo:hi].bitcast(FP8X4),
+                rhs_scale=scales[h, a][:, lo:hi],
+                start=(a == 0),
+                stop=(a == PASSES - 1 and hi == HALF),
+            )
+
+        gate = {}
+        res = {}
+        pair = {}
+
+        def open_banks(h):
+            for m in range(M_TILES):
+                g[h, m] = psum.tile([P, HALF], F32, name="g_%d_%d" % (h, m), tag="g_%d" % m)
+                u[h, m] = psum.tile([P, HALF], F32, name="u_%d_%d" % (h, m), tag="u_%d" % m)
+                gate[h, m] = keep.tile([P, HALF], F32, align_bytes=64, name="gate_%d_%d" % (h, m))
+                if h == 1:
+                    res[h, m] = keep.tile([P, HALF], F32, align_bytes=64, name="res_%d_%d" % (h, m))
+            if h == 0:
+                for m in (0, 2):
+                    t = keep.tile([P, 2, HALF], F32, align_bytes=64, name="res_%d_%d" % (h, m))
+                    pair[m] = t
+                    res[h, m] = t[:, 0, :]
+                    res[h, m + 1] = t[:, 1, :]
+
+        def silu(h, m, lo=0, hi=HALF):
+            nc.scalar.activation(out=gate[h, m][:, lo:hi], in_=g[h, m][:, lo:hi], func=ACT.Silu)
+
+        def mul(h, m, lo=0, hi=HALF):
+            nc.vector.tensor_tensor(
+                out=res[h, m][:, lo:hi], in0=u[h, m][:, lo:hi], in1=gate[h, m][:, lo:hi], op=ALU.mult
+            )
+
+        def store(h, m, lo=0, hi=HALF):
+            nc.sync.dma_start(
+                out=out[128 * m : 128 * (m + 1), HALF * h + lo : HALF * h + hi], in_=res[h, m][:, lo:hi]
+            )
+
+        def multiply(h, a):
+            for m in range(M_TILES):
+                pass_g(h, a, m, 0, HALF)
+                pass_u(h, a, m, 0, HALF)
+
+        def multiply_u_first(h, a):
+            for m in range(M_TILES):
+                pass_u(h, a, m, 0, HALF)
+            for m in range(M_TILES):
+                pass_g(h, a, m, 0, HALF)
+
+        def multiply_g_first(h, a):
+            for m in range(M_TILES):
+                pass_g(h, a, m, 0, HALF)
+            for m in range(M_TILES):
+                pass_u(h, a, m, 0, HALF)
+
+        def multiply_g_first(h, a):
+            for m in range(M_TILES):
+                pass_g(h, a, m, 0, HALF)
+            for m in range(M_TILES):
+                pass_u(h, a, m, 0, HALF)
+
+        open_banks(0)
+        prepare_pieces(0, 0)
+        multiply_u_first(0, 0)
+        for a in range(1, PASSES):
+            copies_whole(0, a)
+            quantize(0, a, 0)
+            quantize(0, a, 256)
+            if a == 1:
+                multiply_u_first(0, a)
+            else:
+                multiply_g_first(0, a)
+
+        open_banks(1)
+        prepare_pieces(1, 0)
+        tiles(1, 1)
+        silu(0, 0)
+        mul(0, 0)
+        silu(0, 1)
+        mul(0, 1)
+        silu(0, 2)
+        silu(0, 3)
+        copy_piece_v(1, 1, 0)
+        copy_piece_s(1, 1, 0)
+        mul(0, 2)
+        quantize(1, 1, 0)
+        copy_piece_v(1, 1, 256)
+        copy_piece_s(1, 1, 256)
+        mul(0, 3)
+        quantize(1, 1, 256)
+        multiply(1, 0)
+        multiply(1, 1)
+        prepare_pieces(1, 2)
+        multiply(1, 2)
+        prepare_pieces(1, 3)
+        for m in (0, 1):
+            pass_g(1, 3, m, 0, HALF)
+            pass_u(1, 3, m, 0, HALF)
+        for m in (2, 3):
+            pass_g(1, 3, m, 0, HALF)
+        for m in (2, 3):
+            pass_u(1, 3, m, 0, HALF)
+        for m in (0, 2):
+            nc.sync.dma_start(
+                out=out[128 * m : 128 * (m + 2), 0:HALF].rearrange("(m p) w -> p m w", p=P), in_=pair[m][:]
+            )
+        for m in range(M_TILES - 1):
+            silu(1, m)
+            mul(1, m)
+            store(1, m)
+        for lo in (0, 256):
+            silu(1, 3, lo, lo + 256)
+            mul(1, 3, lo, lo + 256)
+            store(1, 3, lo, lo + 256)

@@ -31,31 +31,27 @@ def tile_mix_glu48_fm_none_kernel(tc, x, w4_words, w4_scales, w8_words, w8_scale
 
         sc4 = keep.tile([P, PASSES * M], U8, align_bytes=64, name="sc4")
         sc8 = keep.tile([P, M], U8, align_bytes=64, name="sc8")
-        dummy = keep.tile([P, 8], F32, align_bytes=64, name="dummy")
         nc.vector.memset(sc8[:].bitcast(I32), 0)
         nc.vector.memset(sc4[:].bitcast(I32), 0)
-        nc.vector.memset(dummy[:], 0.0)
 
         raw = {}
         w4 = {}
         w8 = {}
 
-        def load_x(h, a, pieces=1, which=(0, 1)):
-            width = HALF // pieces
-            for c in which[:pieces]:
-                t = keep.tile([P, 4, width], F32, align_bytes=64, name="raw_%d_%d_%d" % (h, a, c))
-                for lo in range(0, width, 256):
-                    raw[h, a, width * c + lo] = t[:, :, lo : lo + 256]
-                nc.sync.dma_start(
-                    out=t[:],
-                    in_=x[512 * a : 512 * (a + 1), HALF * h + width * c : HALF * h + width * (c + 1)].rearrange(
-                        "(p j) w -> p j w", j=4
-                    ),
-                )
+        def load_x(h, a):
+            raw[h, a] = keep.tile([P, 4, HALF], F32, align_bytes=64, name="raw_%d_%d" % (h, a))
+            nc.sync.dma_start(
+                out=raw[h, a][:],
+                in_=x[512 * a : 512 * (a + 1), HALF * h : HALF * (h + 1)].rearrange("(p j) w -> p j w", j=4),
+            )
 
-        def load_w8(a):
-            w8[a] = keep.tile([P, 4 * M], U8, align_bytes=64, name="w8_%d" % a)
-            nc.sync.dma_start(out=w8[a][:].bitcast(I32), in_=w8_words[a].rearrange("p n i -> p (n i)").bitcast(I32))
+        def load_w8(a, n):
+            t = keep.tile([P, n, 4 * M], U8, align_bytes=64, name="w8_%d" % a)
+            for i in range(n):
+                w8[a + i] = t[:, i, :]
+            nc.sync.dma_start(
+                out=t[:].bitcast(I32), in_=w8_words[a : a + n].rearrange("a p n i -> p a (n i)").bitcast(I32)
+            )
 
         def load_w4(a, n):
             t = keep.tile([P, n, 2 * M], U8, align_bytes=64, name="w4_%d" % a)
@@ -65,121 +61,101 @@ def tile_mix_glu48_fm_none_kernel(tc, x, w4_words, w4_scales, w8_words, w8_scale
                 out=t[:].bitcast(I32), in_=w4_words[a : a + n].rearrange("a p b -> p a b").bitcast(I32)
             )
 
-        def load_sc8():
+        def load_sc8(queue):
             for q in range(4):
-                nc.scalar.dma_start(
+                queue.dma_start(
                     out=sc8[32 * q : 32 * q + 16, :].bitcast(I32),
                     in_=w8_scales[:, 4 * q : 4 * q + 4, :].bitcast(I32),
                 )
 
-        def load_sc4():
+        def load_sc4(queue):
             for q in range(4):
-                nc.scalar.dma_start(
+                queue.dma_start(
                     out=sc4[32 * q : 32 * q + 4, :].bitcast(I32).rearrange("r (a n) -> r a n", a=PASSES),
                     in_=w4_scales[:, 4 * q : 4 * q + 4, :].bitcast(I32).rearrange("a r n -> r a n"),
                 )
 
-        load_sc8()
-        nc.scalar.activation(out=dummy[:, 0:1], in_=dummy[:, 1:2], func=ACT.Silu)
-        load_x(0, 0, 2)
-        load_w4(0, 1)
-        load_w8(0)
-        load_x(0, 1)
-        load_sc4()
-        load_w4(1, 3)
-        load_w8(1)
-        load_x(0, 2)
-        load_x(0, 3)
-        load_w8(2)
-        load_x(1, 0, 2)
-        load_w8(3)
-        for a in range(1, PASSES):
-            load_x(1, a, 2)
-
         grouped = {}
         codes = {}
         scales = {}
+        for h in range(2):
+            for a in range(PASSES):
+                grouped[h, a] = keep.tile([P, HALF, 4], BF16, align_bytes=64, name="grouped_%d_%d" % (h, a))
+                codes[h, a] = keep.tile([P, HALF], U32, align_bytes=64, name="codes_%d_%d" % (h, a))
+                scales[h, a] = keep.tile([P, HALF], U8, align_bytes=64, name="scales_%d_%d" % (h, a))
 
         def interleave(engine_copy, h, a, lo, hi):
-            base = lo // 256 * 256
             engine_copy(
                 out=grouped[h, a][:, lo:hi, :].rearrange("p (c i) t -> p c t i", i=4),
-                in_=raw[h, a, base][:, :, lo - base : hi - base].rearrange("p t (c i) -> p c t i", i=4),
+                in_=raw[h, a][:, :, lo:hi].rearrange("p t (c i) -> p c t i", i=4),
             )
 
-        def tiles(h, a):
-            grouped[h, a] = keep.tile([P, HALF, 4], BF16, align_bytes=64, name="grouped_%d_%d" % (h, a))
-            codes[h, a] = keep.tile([P, HALF], U32, align_bytes=64, name="codes_%d_%d" % (h, a))
-            scales[h, a] = keep.tile([P, HALF], U8, align_bytes=64, name="scales_%d_%d" % (h, a))
+        def copy_v(h, a, lo, hi):
+            interleave(nc.vector.tensor_copy, h, a, lo, hi)
 
-        def quantize(h, a, lo):
-            nc.vector.quantize_mx(
-                out=codes[h, a][:, lo : lo + 256].bitcast(FP8X4),
-                scales=scales[h, a][:, lo : lo + 256],
-                in_=grouped[h, a][:, lo : lo + 256, :].rearrange("p w t -> p (w t)"),
-            )
+        def copy_s(h, a, lo, hi):
+            interleave(nc.scalar.copy, h, a, lo, hi)
 
-        def copies_whole(h, a):
-            tiles(h, a)
-            interleave(nc.vector.tensor_copy, h, a, 0, 256)
-            interleave(nc.vector.tensor_copy, h, a, 256, V_COLS)
-            interleave(nc.scalar.copy, h, a, V_COLS, HALF)
-
-        def copy_piece_v(h, a, lo):
-            interleave(nc.vector.tensor_copy, h, a, lo, lo + V_COLS // 2)
-
-        def copy_piece_s(h, a, lo):
-            interleave(nc.scalar.copy, h, a, lo + V_COLS // 2, lo + 256)
-
-        def prepare_pieces(h, a):
-            tiles(h, a)
+        def quantize(h, a):
             for lo in (0, 256):
-                copy_piece_v(h, a, lo)
-                copy_piece_s(h, a, lo)
-                quantize(h, a, lo)
+                nc.vector.quantize_mx(
+                    out=codes[h, a][:, lo : lo + 256].bitcast(FP8X4),
+                    scales=scales[h, a][:, lo : lo + 256],
+                    in_=grouped[h, a][:, lo : lo + 256, :].rearrange("p w t -> p (w t)"),
+                )
+
+        def prepare(h, a, v_cols=V_COLS):
+            copy_v(h, a, 0, 256)
+            copy_v(h, a, 256, v_cols)
+            if v_cols < HALF:
+                copy_s(h, a, v_cols, HALF)
+            quantize(h, a)
 
         g = {}
         u = {}
 
-        def pass_g(h, a, m, lo, hi):
+        def pass_g(h, a, m):
+            if a == 0:
+                g[h, m] = psum.tile([P, HALF], F32, name="g_%d_%d" % (h, m), tag="g_%d" % m)
             nc.tensor.matmul_mx(
-                out=g[h, m][:, lo:hi],
+                out=g[h, m][:],
                 lhsT=w4[a][:, 256 * m : 256 * (m + 1)].bitcast(FP4X4),
                 lhsT_scale=sc4[:, M * a + 128 * m : M * a + 128 * (m + 1)],
-                rhs=codes[h, a][:, lo:hi].bitcast(FP8X4),
-                rhs_scale=scales[h, a][:, lo:hi],
+                rhs=codes[h, a][:].bitcast(FP8X4),
+                rhs_scale=scales[h, a][:],
                 start=(a == 0),
-                stop=(a == PASSES - 1 and hi == HALF),
+                stop=(a == PASSES - 1),
             )
 
-        def pass_u(h, a, m, lo, hi):
+        def pass_u(h, a, m):
+            if a == 0:
+                u[h, m] = psum.tile([P, HALF], F32, name="u_%d_%d" % (h, m), tag="u_%d" % m)
             nc.tensor.matmul_mx(
-                out=u[h, m][:, lo:hi],
+                out=u[h, m][:],
                 lhsT=w8[a][:, 512 * m : 512 * (m + 1)].bitcast(FP8X4),
                 lhsT_scale=sc8[4 * a : P, 128 * m : 128 * (m + 1)],
-                rhs=codes[h, a][:, lo:hi].bitcast(FP8X4),
-                rhs_scale=scales[h, a][:, lo:hi],
+                rhs=codes[h, a][:].bitcast(FP8X4),
+                rhs_scale=scales[h, a][:],
                 start=(a == 0),
-                stop=(a == PASSES - 1 and hi == HALF),
+                stop=(a == PASSES - 1),
             )
+
+        def passes_g(h, a):
+            for m in range(M_TILES):
+                pass_g(h, a, m)
+
+        def passes_u(h, a):
+            for m in range(M_TILES):
+                pass_u(h, a, m)
 
         gate = {}
         res = {}
-        pair = {}
-
-        def open_banks(h):
-            for m in range(M_TILES):
-                g[h, m] = psum.tile([P, HALF], F32, name="g_%d_%d" % (h, m), tag="g_%d" % m)
-                u[h, m] = psum.tile([P, HALF], F32, name="u_%d_%d" % (h, m), tag="u_%d" % m)
+        first = keep.tile([P, M_TILES, HALF], F32, align_bytes=64, name="first")
+        for m in range(M_TILES):
+            res[0, m] = first[:, m, :]
+            res[1, m] = keep.tile([P, HALF], F32, align_bytes=64, name="res_%d" % m)
+            for h in range(2):
                 gate[h, m] = keep.tile([P, HALF], F32, align_bytes=64, name="gate_%d_%d" % (h, m))
-                if h == 1:
-                    res[h, m] = keep.tile([P, HALF], F32, align_bytes=64, name="res_%d_%d" % (h, m))
-            if h == 0:
-                for m in (0, 2):
-                    t = keep.tile([P, 2, HALF], F32, align_bytes=64, name="res_%d_%d" % (h, m))
-                    pair[m] = t
-                    res[h, m] = t[:, 0, :]
-                    res[h, m + 1] = t[:, 1, :]
 
         def silu(h, m, lo=0, hi=HALF):
             nc.scalar.activation(out=gate[h, m][:, lo:hi], in_=g[h, m][:, lo:hi], func=ACT.Silu)
@@ -189,84 +165,58 @@ def tile_mix_glu48_fm_none_kernel(tc, x, w4_words, w4_scales, w8_words, w8_scale
                 out=res[h, m][:, lo:hi], in0=u[h, m][:, lo:hi], in1=gate[h, m][:, lo:hi], op=ALU.mult
             )
 
-        def store(h, m, lo=0, hi=HALF):
-            nc.sync.dma_start(
-                out=out[128 * m : 128 * (m + 1), HALF * h + lo : HALF * h + hi], in_=res[h, m][:, lo:hi]
-            )
+        def store(m, lo=0, hi=HALF):
+            nc.sync.dma_start(out=out[128 * m : 128 * (m + 1), HALF + lo : HALF + hi], in_=res[1, m][:, lo:hi])
 
-        def multiply(h, a):
-            for m in range(M_TILES):
-                pass_g(h, a, m, 0, HALF)
-                pass_u(h, a, m, 0, HALF)
-
-        def multiply_u_first(h, a):
-            for m in range(M_TILES):
-                pass_u(h, a, m, 0, HALF)
-            for m in range(M_TILES):
-                pass_g(h, a, m, 0, HALF)
-
-        def multiply_g_first(h, a):
-            for m in range(M_TILES):
-                pass_g(h, a, m, 0, HALF)
-            for m in range(M_TILES):
-                pass_u(h, a, m, 0, HALF)
-
-        def multiply_g_first(h, a):
-            for m in range(M_TILES):
-                pass_g(h, a, m, 0, HALF)
-            for m in range(M_TILES):
-                pass_u(h, a, m, 0, HALF)
-
-        open_banks(0)
-        prepare_pieces(0, 0)
-        multiply_u_first(0, 0)
+        load_sc8(nc.scalar)
+        load_x(0, 0)
+        load_w8(0, 3)
+        load_w4(0, 3)
+        load_sc4(nc.sync)
         for a in range(1, PASSES):
-            copies_whole(0, a)
-            quantize(0, a, 0)
-            quantize(0, a, 256)
-            if a == 1:
-                multiply_u_first(0, a)
-            else:
-                multiply_g_first(0, a)
+            load_x(0, a)
+        load_w4(3, 1)
+        load_w8(3, 1)
+        for a in range(PASSES):
+            load_x(1, a)
 
-        open_banks(1)
-        prepare_pieces(1, 0)
-        tiles(1, 1)
-        silu(0, 0)
+        for a in range(PASSES - 1):
+            prepare(0, a)
+            passes_u(0, a)
+            passes_g(0, a)
+        prepare(0, 3, HALF)
+        for m in range(M_TILES):
+            pass_g(0, 3, m)
+            pass_u(0, 3, m)
+
+        for m in range(M_TILES):
+            silu(0, m)
         mul(0, 0)
-        silu(0, 1)
-        mul(0, 1)
-        silu(0, 2)
-        silu(0, 3)
-        copy_piece_v(1, 1, 0)
-        copy_piece_s(1, 1, 0)
-        mul(0, 2)
-        quantize(1, 1, 0)
-        copy_piece_v(1, 1, 256)
-        copy_piece_s(1, 1, 256)
-        mul(0, 3)
-        quantize(1, 1, 256)
-        multiply(1, 0)
-        multiply(1, 1)
-        prepare_pieces(1, 2)
-        multiply(1, 2)
-        prepare_pieces(1, 3)
-        for m in (0, 1):
-            pass_g(1, 3, m, 0, HALF)
-            pass_u(1, 3, m, 0, HALF)
-        for m in (2, 3):
-            pass_g(1, 3, m, 0, HALF)
-        for m in (2, 3):
-            pass_u(1, 3, m, 0, HALF)
-        for m in (0, 2):
-            nc.sync.dma_start(
-                out=out[128 * m : 128 * (m + 2), 0:HALF].rearrange("(m p) w -> p m w", p=P), in_=pair[m][:]
-            )
+        prepare(1, 0, HALF)
+        passes_g(1, 0)
+        pass_u(1, 0, 0)
+        for m in range(1, M_TILES):
+            mul(0, m)
+            pass_u(1, 0, m)
+        copy_v(1, 1, 0, 192)
+        copy_s(1, 1, 192, HALF)
+        quantize(1, 1)
+        passes_g(1, 1)
+        passes_u(1, 1)
+        prepare(1, 2)
+        passes_g(1, 2)
+        passes_u(1, 2)
+        prepare(1, 3)
+        for m in range(M_TILES):
+            pass_g(1, 3, m)
+            pass_u(1, 3, m)
+
+        nc.sync.dma_start(out=out[:, 0:HALF].rearrange("(m p) w -> p m w", p=P), in_=first[:])
         for m in range(M_TILES - 1):
             silu(1, m)
             mul(1, m)
-            store(1, m)
+            store(m)
         for lo in (0, 256):
             silu(1, 3, lo, lo + 256)
             mul(1, 3, lo, lo + 256)
-            store(1, 3, lo, lo + 256)
+            store(3, lo, lo + 256)

@@ -38,11 +38,12 @@ def tile_mix_glu48_fm_none_kernel(tc, x, w4_words, w4_scales, w8_words, w8_scale
         w4 = {}
         w8 = {}
 
-        def load_x(h, a):
-            raw[h, a] = keep.tile([P, 4, HALF], F32, align_bytes=64, name="raw_%d_%d" % (h, a))
+        def load_x(h, a, lo=0, hi=HALF):
+            t = keep.tile([P, 4, hi - lo], F32, align_bytes=64, name="raw_%d_%d_%d" % (h, a, lo))
+            raw.setdefault((h, a), []).append((lo, hi, t))
             nc.sync.dma_start(
-                out=raw[h, a][:],
-                in_=x[512 * a : 512 * (a + 1), HALF * h : HALF * (h + 1)].rearrange("(p j) w -> p j w", j=4),
+                out=t[:],
+                in_=x[512 * a : 512 * (a + 1), HALF * h + lo : HALF * h + hi].rearrange("(p j) w -> p j w", j=4),
             )
 
         def load_w8(a, n):
@@ -85,9 +86,10 @@ def tile_mix_glu48_fm_none_kernel(tc, x, w4_words, w4_scales, w8_words, w8_scale
                 scales[h, a] = keep.tile([P, HALF], U8, align_bytes=64, name="scales_%d_%d" % (h, a))
 
         def interleave(engine_copy, h, a, lo, hi):
+            base, t = [(b, t) for b, e, t in raw[h, a] if b <= lo and hi <= e][0]
             engine_copy(
                 out=grouped[h, a][:, lo:hi, :].rearrange("p (c i) t -> p c t i", i=4),
-                in_=raw[h, a][:, :, lo:hi].rearrange("p t (c i) -> p c t i", i=4),
+                in_=t[:, :, lo - base : hi - base].rearrange("p t (c i) -> p c t i", i=4),
             )
 
         def copy_v(h, a, lo, hi):
@@ -96,13 +98,16 @@ def tile_mix_glu48_fm_none_kernel(tc, x, w4_words, w4_scales, w8_words, w8_scale
         def copy_s(h, a, lo, hi):
             interleave(nc.scalar.copy, h, a, lo, hi)
 
+        def quant(h, a, lo, hi):
+            nc.vector.quantize_mx(
+                out=codes[h, a][:, lo:hi].bitcast(FP8X4),
+                scales=scales[h, a][:, lo:hi],
+                in_=grouped[h, a][:, lo:hi, :].rearrange("p w t -> p (w t)"),
+            )
+
         def quantize(h, a):
-            for lo in (0, 256):
-                nc.vector.quantize_mx(
-                    out=codes[h, a][:, lo : lo + 256].bitcast(FP8X4),
-                    scales=scales[h, a][:, lo : lo + 256],
-                    in_=grouped[h, a][:, lo : lo + 256, :].rearrange("p w t -> p (w t)"),
-                )
+            quant(h, a, 0, 256)
+            quant(h, a, 256, HALF)
 
         def prepare(h, a, v_cols=V_COLS):
             copy_v(h, a, 0, 256)
@@ -114,30 +119,30 @@ def tile_mix_glu48_fm_none_kernel(tc, x, w4_words, w4_scales, w8_words, w8_scale
         g = {}
         u = {}
 
-        def pass_g(h, a, m):
+        def pass_g(h, a, m, lo=0, hi=HALF):
             if a == 0:
                 g[h, m] = psum.tile([P, HALF], F32, name="g_%d_%d" % (h, m), tag="g_%d" % m)
             nc.tensor.matmul_mx(
-                out=g[h, m][:],
+                out=g[h, m][:, lo:hi],
                 lhsT=w4[a][:, 256 * m : 256 * (m + 1)].bitcast(FP4X4),
                 lhsT_scale=sc4[:, M * a + 128 * m : M * a + 128 * (m + 1)],
-                rhs=codes[h, a][:].bitcast(FP8X4),
-                rhs_scale=scales[h, a][:],
+                rhs=codes[h, a][:, lo:hi].bitcast(FP8X4),
+                rhs_scale=scales[h, a][:, lo:hi],
                 start=(a == 0),
-                stop=(a == PASSES - 1),
+                stop=(a == PASSES - 1 and hi == HALF),
             )
 
-        def pass_u(h, a, m):
+        def pass_u(h, a, m, lo=0, hi=HALF):
             if a == 0:
                 u[h, m] = psum.tile([P, HALF], F32, name="u_%d_%d" % (h, m), tag="u_%d" % m)
             nc.tensor.matmul_mx(
-                out=u[h, m][:],
+                out=u[h, m][:, lo:hi],
                 lhsT=w8[a][:, 512 * m : 512 * (m + 1)].bitcast(FP8X4),
                 lhsT_scale=sc8[4 * a : P, 128 * m : 128 * (m + 1)],
-                rhs=codes[h, a][:].bitcast(FP8X4),
-                rhs_scale=scales[h, a][:],
+                rhs=codes[h, a][:, lo:hi].bitcast(FP8X4),
+                rhs_scale=scales[h, a][:, lo:hi],
                 start=(a == 0),
-                stop=(a == PASSES - 1),
+                stop=(a == PASSES - 1 and hi == HALF),
             )
 
         def passes_g(h, a):
@@ -165,58 +170,100 @@ def tile_mix_glu48_fm_none_kernel(tc, x, w4_words, w4_scales, w8_words, w8_scale
                 out=res[h, m][:, lo:hi], in0=u[h, m][:, lo:hi], in1=gate[h, m][:, lo:hi], op=ALU.mult
             )
 
+        def store_first():
+            nc.sync.dma_start(out=out[:, 0:HALF].rearrange("(m p) w -> p m w", p=P), in_=first[:])
+
         def store(m, lo=0, hi=HALF):
             nc.sync.dma_start(out=out[128 * m : 128 * (m + 1), HALF + lo : HALF + hi], in_=res[1, m][:, lo:hi])
 
         load_sc8(nc.scalar)
-        load_x(0, 0)
-        load_w8(0, 3)
-        load_w4(0, 3)
-        load_sc4(nc.sync)
-        for a in range(1, PASSES):
-            load_x(0, a)
+        load_x(0, 0, 0, 256)
+        load_x(0, 0, 256, HALF)
+        load_w8(0, 1)
+        load_x(0, 1)
+        load_sc4(nc.scalar)
+        load_w4(0, 2)
+        load_w8(1, 1)
+        load_x(0, 2)
+        load_w8(2, 1)
+        load_w4(2, 1)
+        load_x(0, 3, 0, 256)
+        load_x(0, 3, 256, HALF)
         load_w4(3, 1)
+        load_x(1, 0, 0, 256)
+        load_x(1, 0, 256, HALF)
         load_w8(3, 1)
-        for a in range(PASSES):
-            load_x(1, a)
+        for a in range(1, PASSES):
+            load_x(1, a, 0, 256)
+            load_x(1, a, 256, HALF)
 
-        for a in range(PASSES - 1):
+        def piece(h, a, lo):
+            copy_v(h, a, lo, lo + 160)
+            copy_s(h, a, lo + 160, lo + 256)
+            quant(h, a, lo, lo + 256)
+
+        for lo in (0, 256):
+            copy_v(0, 0, lo, lo + 256)
+            quant(0, 0, lo, lo + 256)
+        passes_u(0, 0)
+        passes_g(0, 0)
+        for a in (1, 2):
             prepare(0, a)
             passes_u(0, a)
             passes_g(0, a)
-        prepare(0, 3, HALF)
-        for m in range(M_TILES):
-            pass_g(0, 3, m)
-            pass_u(0, 3, m)
+        piece(0, 3, 0)
+        copy_v(0, 3, 256, HALF)
+        quant(0, 3, 256, HALF)
+        passes_g(0, 3)
+        passes_u(0, 3)
 
         for m in range(M_TILES):
             silu(0, m)
-        mul(0, 0)
-        prepare(1, 0, HALF)
+        for lo in (0, 256):
+            copy_v(1, 0, lo, lo + 256)
+            quant(1, 0, lo, lo + 256)
         passes_g(1, 0)
-        pass_u(1, 0, 0)
-        for m in range(1, M_TILES):
+        for m in range(2):
             mul(0, m)
             pass_u(1, 0, m)
-        copy_v(1, 1, 0, 192)
-        copy_s(1, 1, 192, HALF)
-        quantize(1, 1)
-        passes_g(1, 1)
-        passes_u(1, 1)
-        prepare(1, 2)
-        passes_g(1, 2)
-        passes_u(1, 2)
-        prepare(1, 3)
+        copy_v(1, 1, 0, 96)
+        copy_s(1, 1, 96, 256)
+        quant(1, 1, 0, 256)
+        for m in range(M_TILES):
+            pass_g(1, 1, m, 0, 128)
+            pass_g(1, 1, m, 128, 256)
+        for m in range(2):
+            pass_u(1, 1, m, 0, 256)
+        copy_s(1, 1, 256, HALF)
+        for m in range(2, M_TILES):
+            mul(0, m)
+            pass_u(1, 0, m)
+            pass_u(1, 1, m, 0, 256)
+        quant(1, 1, 256, HALF)
+        for m in range(M_TILES):
+            pass_g(1, 1, m, 256, 384)
+            pass_g(1, 1, m, 384, HALF)
+            pass_u(1, 1, m, 256, HALF)
+        copy_v(1, 2, 0, 128)
+        copy_s(1, 2, 128, 256)
+        copy_v(1, 2, 256, 416)
+        copy_s(1, 2, 416, HALF)
+        quantize(1, 2)
+        for m in range(M_TILES):
+            pass_g(1, 2, m)
+            pass_u(1, 2, m)
+        piece(1, 3, 0)
+        piece(1, 3, 256)
         for m in range(M_TILES):
             pass_g(1, 3, m)
             pass_u(1, 3, m)
 
-        nc.sync.dma_start(out=out[:, 0:HALF].rearrange("(m p) w -> p m w", p=P), in_=first[:])
-        for m in range(M_TILES - 1):
-            silu(1, m)
-            mul(1, m)
-            store(m)
-        for lo in (0, 256):
-            silu(1, 3, lo, lo + 256)
-            mul(1, 3, lo, lo + 256)
-            store(3, lo, lo + 256)
+        store_first()
+        for m in range(M_TILES):
+            for lo in (0, 256):
+                silu(1, m, lo, lo + 256)
+                mul(1, m, lo, lo + 256)
+                if m == M_TILES - 1:
+                    store(m, lo, lo + 256)
+            if m < M_TILES - 1:
+                store(m)

@@ -17,9 +17,17 @@ ALU = mybir.AluOpType
 
 P = 128
 PASSES = K // 512
+LAST = PASSES - 1
 HALF = 512
-M_TILES = M // 128
-V_COLS = 320
+SIDE = 256
+NARROW = 128
+ROW_TILES = M // P
+OWN = (0, 1)
+SHARED = (2, 3)
+V_OF_HALF = 320
+V_OF_SIDE = 160
+V_BETWEEN_PRODUCTS = 96
+V_AFTER_PRODUCTS = 128
 
 
 def tile_mix_glu48_fm_none_kernel(tc, x, w4_words, w4_scales, w8_words, w8_scales, out):
@@ -38,40 +46,38 @@ def tile_mix_glu48_fm_none_kernel(tc, x, w4_words, w4_scales, w8_words, w8_scale
         w4 = {}
         w8 = {}
 
-        def load_x(h, a, lo=0, hi=HALF):
-            t = keep.tile([P, 4, hi - lo], F32, align_bytes=64, name="raw_%d_%d_%d" % (h, a, lo))
-            raw.setdefault((h, a), []).append((lo, hi, t))
+        def load_x(h, a, cuts):
+            for lo, hi in zip(cuts, cuts[1:]):
+                piece = keep.tile([P, 4, hi - lo], F32, align_bytes=64, name="raw_%d_%d_%d" % (h, a, lo))
+                raw.setdefault((h, a), []).append((lo, hi, piece))
+                nc.sync.dma_start(
+                    out=piece[:],
+                    in_=x[512 * a : 512 * (a + 1), HALF * h + lo : HALF * h + hi].rearrange("(p j) w -> p j w", j=4),
+                )
+
+        def load_w8(a):
+            w8[a] = keep.tile([P, 4 * M], U8, align_bytes=64, name="w8_%d" % a)
+            nc.sync.dma_start(out=w8[a][:].bitcast(I32), in_=w8_words[a].rearrange("p n i -> p (n i)").bitcast(I32))
+
+        def load_w4(first, count):
+            words = keep.tile([P, count, 2 * M], U8, align_bytes=64, name="w4_%d" % first)
+            for i in range(count):
+                w4[first + i] = words[:, i, :]
             nc.sync.dma_start(
-                out=t[:],
-                in_=x[512 * a : 512 * (a + 1), HALF * h + lo : HALF * h + hi].rearrange("(p j) w -> p j w", j=4),
+                out=words[:].bitcast(I32),
+                in_=w4_words[first : first + count].rearrange("a p b -> p a b").bitcast(I32),
             )
 
-        def load_w8(a, n):
-            t = keep.tile([P, n, 4 * M], U8, align_bytes=64, name="w8_%d" % a)
-            for i in range(n):
-                w8[a + i] = t[:, i, :]
-            nc.sync.dma_start(
-                out=t[:].bitcast(I32), in_=w8_words[a : a + n].rearrange("a p n i -> p a (n i)").bitcast(I32)
-            )
-
-        def load_w4(a, n):
-            t = keep.tile([P, n, 2 * M], U8, align_bytes=64, name="w4_%d" % a)
-            for i in range(n):
-                w4[a + i] = t[:, i, :]
-            nc.sync.dma_start(
-                out=t[:].bitcast(I32), in_=w4_words[a : a + n].rearrange("a p b -> p a b").bitcast(I32)
-            )
-
-        def load_sc8(queue):
+        def load_sc8():
             for q in range(4):
-                queue.dma_start(
+                nc.scalar.dma_start(
                     out=sc8[32 * q : 32 * q + 16, :].bitcast(I32),
                     in_=w8_scales[:, 4 * q : 4 * q + 4, :].bitcast(I32),
                 )
 
-        def load_sc4(queue):
+        def load_sc4():
             for q in range(4):
-                queue.dma_start(
+                nc.scalar.dma_start(
                     out=sc4[32 * q : 32 * q + 4, :].bitcast(I32).rearrange("r (a n) -> r a n", a=PASSES),
                     in_=w4_scales[:, 4 * q : 4 * q + 4, :].bitcast(I32).rearrange("a r n -> r a n"),
                 )
@@ -86,10 +92,10 @@ def tile_mix_glu48_fm_none_kernel(tc, x, w4_words, w4_scales, w8_words, w8_scale
                 scales[h, a] = keep.tile([P, HALF], U8, align_bytes=64, name="scales_%d_%d" % (h, a))
 
         def interleave(engine_copy, h, a, lo, hi):
-            base, t = [(b, t) for b, e, t in raw[h, a] if b <= lo and hi <= e][0]
+            base, piece = [(begin, tile) for begin, end, tile in raw[h, a] if begin <= lo and hi <= end][0]
             engine_copy(
-                out=grouped[h, a][:, lo:hi, :].rearrange("p (c i) t -> p c t i", i=4),
-                in_=t[:, :, lo - base : hi - base].rearrange("p t (c i) -> p c t i", i=4),
+                out=grouped[h, a][:, lo:hi, :].rearrange("p (c i) j -> p c j i", i=4),
+                in_=piece[:, :, lo - base : hi - base].rearrange("p j (c i) -> p c j i", i=4),
             )
 
         def copy_v(h, a, lo, hi):
@@ -98,172 +104,195 @@ def tile_mix_glu48_fm_none_kernel(tc, x, w4_words, w4_scales, w8_words, w8_scale
         def copy_s(h, a, lo, hi):
             interleave(nc.scalar.copy, h, a, lo, hi)
 
-        def quant(h, a, lo, hi):
+        def quantize(h, a, lo, hi):
             nc.vector.quantize_mx(
                 out=codes[h, a][:, lo:hi].bitcast(FP8X4),
                 scales=scales[h, a][:, lo:hi],
-                in_=grouped[h, a][:, lo:hi, :].rearrange("p w t -> p (w t)"),
+                in_=grouped[h, a][:, lo:hi, :].rearrange("p w j -> p (w j)"),
             )
 
-        def quantize(h, a):
-            quant(h, a, 0, 256)
-            quant(h, a, 256, HALF)
+        def side_shared(h, a, side, v_cols=V_OF_SIDE):
+            lo = SIDE * side
+            copy_v(h, a, lo, lo + v_cols)
+            copy_s(h, a, lo + v_cols, lo + SIDE)
+            quantize(h, a, lo, lo + SIDE)
 
-        def prepare(h, a, v_cols=V_COLS):
-            copy_v(h, a, 0, 256)
-            copy_v(h, a, 256, v_cols)
-            if v_cols < HALF:
-                copy_s(h, a, v_cols, HALF)
-            quantize(h, a)
+        def side_on_vector(h, a, side):
+            copy_v(h, a, SIDE * side, SIDE * (side + 1))
+            quantize(h, a, SIDE * side, SIDE * (side + 1))
 
-        g = {}
-        u = {}
+        def chunk_shared(h, a):
+            copy_v(h, a, 0, SIDE)
+            copy_v(h, a, SIDE, V_OF_HALF)
+            copy_s(h, a, V_OF_HALF, HALF)
+            quantize(h, a, 0, SIDE)
+            quantize(h, a, SIDE, HALF)
+
+        banks = {}
+        filled = {}
+
+        def place(h, m, lo):
+            if h == 1 and m in SHARED:
+                return SHARED[lo // SIDE], SIDE * SHARED.index(m) + lo % SIDE
+            return m, lo
+
+        def sums(kind, h, m, lo, hi):
+            bank, at = place(h, m, lo)
+            return banks[kind, h, bank][:, at : at + hi - lo]
+
+        def multiply(kind, h, a, m, lo, hi, words, word_scales):
+            key = (kind, h, place(h, m, lo)[0])
+            if key not in banks:
+                banks[key] = psum.tile([P, HALF], F32, name="%s_%d_%d" % key, tag="%s_%d" % (kind, key[2]))
+            before = filled.get(key, 0)
+            filled[key] = before + hi - lo
+            nc.tensor.matmul_mx(
+                out=sums(kind, h, m, lo, hi),
+                lhsT=words,
+                lhsT_scale=word_scales,
+                rhs=codes[h, a][:, lo:hi].bitcast(FP8X4),
+                rhs_scale=scales[h, a][:, lo:hi],
+                start=(before == 0),
+                stop=(filled[key] == PASSES * HALF),
+            )
 
         def pass_g(h, a, m, lo=0, hi=HALF):
-            if a == 0:
-                g[h, m] = psum.tile([P, HALF], F32, name="g_%d_%d" % (h, m), tag="g_%d" % m)
-            nc.tensor.matmul_mx(
-                out=g[h, m][:, lo:hi],
-                lhsT=w4[a][:, 256 * m : 256 * (m + 1)].bitcast(FP4X4),
-                lhsT_scale=sc4[:, M * a + 128 * m : M * a + 128 * (m + 1)],
-                rhs=codes[h, a][:, lo:hi].bitcast(FP8X4),
-                rhs_scale=scales[h, a][:, lo:hi],
-                start=(a == 0),
-                stop=(a == PASSES - 1 and hi == HALF),
-            )
+            words = w4[a][:, 2 * P * m : 2 * P * (m + 1)].bitcast(FP4X4)
+            multiply("g", h, a, m, lo, hi, words, sc4[:, M * a + P * m : M * a + P * (m + 1)])
 
         def pass_u(h, a, m, lo=0, hi=HALF):
-            if a == 0:
-                u[h, m] = psum.tile([P, HALF], F32, name="u_%d_%d" % (h, m), tag="u_%d" % m)
-            nc.tensor.matmul_mx(
-                out=u[h, m][:, lo:hi],
-                lhsT=w8[a][:, 512 * m : 512 * (m + 1)].bitcast(FP8X4),
-                lhsT_scale=sc8[4 * a : P, 128 * m : 128 * (m + 1)],
-                rhs=codes[h, a][:, lo:hi].bitcast(FP8X4),
-                rhs_scale=scales[h, a][:, lo:hi],
-                start=(a == 0),
-                stop=(a == PASSES - 1 and hi == HALF),
-            )
+            words = w8[a][:, 4 * P * m : 4 * P * (m + 1)].bitcast(FP8X4)
+            multiply("u", h, a, m, lo, hi, words, sc8[4 * a : P, P * m : P * (m + 1)])
 
         def passes_g(h, a):
-            for m in range(M_TILES):
+            for m in range(ROW_TILES):
                 pass_g(h, a, m)
 
         def passes_u(h, a):
-            for m in range(M_TILES):
+            for m in range(ROW_TILES):
                 pass_u(h, a, m)
+
+        def shared_g(a, side):
+            for lo in range(SIDE * side, SIDE * (side + 1), NARROW):
+                for m in SHARED:
+                    pass_g(1, a, m, lo, lo + NARROW)
+
+        def shared_u(a, side):
+            for m in SHARED:
+                pass_u(1, a, m, SIDE * side, SIDE * (side + 1))
 
         gate = {}
         res = {}
-        first = keep.tile([P, M_TILES, HALF], F32, align_bytes=64, name="first")
-        for m in range(M_TILES):
-            res[0, m] = first[:, m, :]
+        first_half = keep.tile([P, ROW_TILES, HALF], F32, align_bytes=64, name="first_half")
+        for m in range(ROW_TILES):
+            res[0, m] = first_half[:, m, :]
             res[1, m] = keep.tile([P, HALF], F32, align_bytes=64, name="res_%d" % m)
             for h in range(2):
                 gate[h, m] = keep.tile([P, HALF], F32, align_bytes=64, name="gate_%d_%d" % (h, m))
 
         def silu(h, m, lo=0, hi=HALF):
-            nc.scalar.activation(out=gate[h, m][:, lo:hi], in_=g[h, m][:, lo:hi], func=ACT.Silu)
+            nc.scalar.activation(out=gate[h, m][:, lo:hi], in_=sums("g", h, m, lo, hi), func=ACT.Silu)
 
-        def mul(h, m, lo=0, hi=HALF):
+        def product(h, m, lo=0, hi=HALF):
             nc.vector.tensor_tensor(
-                out=res[h, m][:, lo:hi], in0=u[h, m][:, lo:hi], in1=gate[h, m][:, lo:hi], op=ALU.mult
+                out=res[h, m][:, lo:hi], in0=sums("u", h, m, lo, hi), in1=gate[h, m][:, lo:hi], op=ALU.mult
             )
 
-        def store_first():
-            nc.sync.dma_start(out=out[:, 0:HALF].rearrange("(m p) w -> p m w", p=P), in_=first[:])
+        def finish(m, side):
+            lo, hi = SIDE * side, SIDE * (side + 1)
+            silu(1, m, lo, hi)
+            product(1, m, lo, hi)
+            nc.sync.dma_start(out=out[P * m : P * (m + 1), HALF + lo : HALF + hi], in_=res[1, m][:, lo:hi])
 
-        def store(m, lo=0, hi=HALF):
-            nc.sync.dma_start(out=out[128 * m : 128 * (m + 1), HALF + lo : HALF + hi], in_=res[1, m][:, lo:hi])
-
-        load_sc8(nc.scalar)
-        load_x(0, 0, 0, 256)
-        load_x(0, 0, 256, HALF)
-        load_w8(0, 1)
-        load_x(0, 1)
-        load_sc4(nc.scalar)
+        whole = (0, HALF)
+        sides = (0, SIDE, HALF)
+        load_sc8()
+        load_x(0, 0, sides)
+        load_w8(0)
+        load_x(0, 1, whole)
+        load_sc4()
         load_w4(0, 2)
-        load_w8(1, 1)
-        load_x(0, 2)
-        load_w8(2, 1)
+        load_w8(1)
+        load_x(0, 2, whole)
+        load_w8(2)
         load_w4(2, 1)
-        load_x(0, 3, 0, 256)
-        load_x(0, 3, 256, HALF)
-        load_w4(3, 1)
-        load_x(1, 0, 0, 256)
-        load_x(1, 0, 256, HALF)
-        load_w8(3, 1)
-        for a in range(1, PASSES):
-            load_x(1, a, 0, 256)
-            load_x(1, a, 256, HALF)
+        load_x(0, LAST, sides)
+        load_w4(LAST, 1)
+        load_x(1, 0, sides)
+        load_w8(LAST)
+        load_x(1, 1, sides)
+        load_x(1, 2, sides)
+        load_x(1, LAST, (0, SIDE, SIDE + NARROW, HALF))
 
-        def piece(h, a, lo):
-            copy_v(h, a, lo, lo + 160)
-            copy_s(h, a, lo + 160, lo + 256)
-            quant(h, a, lo, lo + 256)
-
-        for lo in (0, 256):
-            copy_v(0, 0, lo, lo + 256)
-            quant(0, 0, lo, lo + 256)
+        side_on_vector(0, 0, 0)
+        side_on_vector(0, 0, 1)
         passes_u(0, 0)
         passes_g(0, 0)
-        for a in (1, 2):
-            prepare(0, a)
+        for a in range(1, LAST):
+            chunk_shared(0, a)
             passes_u(0, a)
             passes_g(0, a)
-        piece(0, 3, 0)
-        copy_v(0, 3, 256, HALF)
-        quant(0, 3, 256, HALF)
-        passes_g(0, 3)
-        passes_u(0, 3)
+        side_shared(0, LAST, 0)
+        side_on_vector(0, LAST, 1)
+        passes_g(0, LAST)
+        passes_u(0, LAST)
 
-        for m in range(M_TILES):
+        for m in range(ROW_TILES):
             silu(0, m)
-        for lo in (0, 256):
-            copy_v(1, 0, lo, lo + 256)
-            quant(1, 0, lo, lo + 256)
-        passes_g(1, 0)
-        for m in range(2):
-            mul(0, m)
+        side_on_vector(1, 0, 0)
+        side_on_vector(1, 0, 1)
+        for m in OWN:
+            pass_g(1, 0, m)
+        shared_g(0, 0)
+        shared_g(0, 1)
+        for m in OWN:
+            product(0, m)
             pass_u(1, 0, m)
-        copy_v(1, 1, 0, 96)
-        copy_s(1, 1, 96, 256)
-        quant(1, 1, 0, 256)
-        for m in range(M_TILES):
-            pass_g(1, 1, m, 0, 128)
-            pass_g(1, 1, m, 128, 256)
-        for m in range(2):
-            pass_u(1, 1, m, 0, 256)
-        copy_s(1, 1, 256, HALF)
-        for m in range(2, M_TILES):
-            mul(0, m)
-            pass_u(1, 0, m)
-            pass_u(1, 1, m, 0, 256)
-        quant(1, 1, 256, HALF)
-        for m in range(M_TILES):
-            pass_g(1, 1, m, 256, 384)
-            pass_g(1, 1, m, 384, HALF)
-            pass_u(1, 1, m, 256, HALF)
-        copy_v(1, 2, 0, 128)
-        copy_s(1, 2, 128, 256)
-        copy_v(1, 2, 256, 416)
-        copy_s(1, 2, 416, HALF)
-        quantize(1, 2)
-        for m in range(M_TILES):
-            pass_g(1, 2, m)
-            pass_u(1, 2, m)
-        piece(1, 3, 0)
-        piece(1, 3, 256)
-        for m in range(M_TILES):
-            pass_g(1, 3, m)
-            pass_u(1, 3, m)
 
-        store_first()
-        for m in range(M_TILES):
-            for lo in (0, 256):
-                silu(1, m, lo, lo + 256)
-                mul(1, m, lo, lo + 256)
-                if m == M_TILES - 1:
-                    store(m, lo, lo + 256)
-            if m < M_TILES - 1:
-                store(m)
+        side_shared(1, 1, 0, V_BETWEEN_PRODUCTS)
+        shared_g(1, 0)
+        for m in OWN:
+            pass_u(1, 1, m, 0, SIDE)
+        copy_s(1, 1, SIDE, HALF)
+        product(0, SHARED[0])
+        shared_u(0, 0)
+        shared_u(1, 0)
+        product(0, SHARED[1])
+        shared_u(0, 1)
+        quantize(1, 1, SIDE, HALF)
+        for m in OWN:
+            pass_g(1, 1, m)
+            pass_u(1, 1, m, SIDE, HALF)
+        shared_g(1, 1)
+        shared_u(1, 1)
+
+        side_shared(1, 2, 0, V_AFTER_PRODUCTS)
+        shared_g(2, 0)
+        shared_u(2, 0)
+        side_shared(1, 2, 1)
+        for m in OWN:
+            pass_g(1, 2, m)
+        shared_g(2, 1)
+
+        side_shared(1, LAST, 0)
+        shared_g(LAST, 0)
+        shared_u(LAST, 0)
+        shared_u(2, 1)
+        copy_s(1, LAST, SIDE, SIDE + NARROW)
+        copy_v(1, LAST, SIDE + NARROW, HALF)
+        quantize(1, LAST, SIDE, SIDE + NARROW)
+        quantize(1, LAST, SIDE + NARROW, HALF)
+        shared_g(LAST, 1)
+        shared_u(LAST, 1)
+        for m in OWN:
+            pass_g(1, LAST, m)
+            pass_u(1, 2, m)
+            pass_u(1, LAST, m)
+
+        nc.sync.dma_start(out=out[:, 0:HALF].rearrange("(m p) w -> p m w", p=P), in_=first_half[:])
+        for side in range(2):
+            for m in SHARED:
+                finish(m, side)
+        for m in OWN:
+            for side in range(2):
+                finish(m, side)

@@ -20,14 +20,10 @@ PASSES = K // 512
 LAST = PASSES - 1
 HALF = 512
 SIDE = 256
-NARROW = 128
 ROW_TILES = M // P
+NARROW = 128
 OWN = (0, 1)
 SHARED = (2, 3)
-V_OF_HALF = 320
-V_OF_SIDE = 160
-V_BETWEEN_PRODUCTS = 96
-V_AFTER_PRODUCTS = 128
 
 
 def tile_mix_glu48_fm_none_kernel(tc, x, w4_words, w4_scales, w8_words, w8_scales, out):
@@ -39,8 +35,8 @@ def tile_mix_glu48_fm_none_kernel(tc, x, w4_words, w4_scales, w8_words, w8_scale
 
         sc4 = keep.tile([P, PASSES * M], U8, align_bytes=64, name="sc4")
         sc8 = keep.tile([P, M], U8, align_bytes=64, name="sc8")
-        nc.vector.memset(sc8[:].bitcast(I32), 0)
         nc.vector.memset(sc4[:].bitcast(I32), 0)
+        nc.vector.memset(sc8[:].bitcast(I32), 0)
 
         raw = {}
         w4 = {}
@@ -55,9 +51,14 @@ def tile_mix_glu48_fm_none_kernel(tc, x, w4_words, w4_scales, w8_words, w8_scale
                     in_=x[512 * a : 512 * (a + 1), HALF * h + lo : HALF * h + hi].rearrange("(p j) w -> p j w", j=4),
                 )
 
-        def load_w8(a):
-            w8[a] = keep.tile([P, 4 * M], U8, align_bytes=64, name="w8_%d" % a)
-            nc.sync.dma_start(out=w8[a][:].bitcast(I32), in_=w8_words[a].rearrange("p n i -> p (n i)").bitcast(I32))
+        def load_w8(first, count):
+            words = keep.tile([P, count, 4 * M], U8, align_bytes=64, name="w8_%d" % first)
+            for i in range(count):
+                w8[first + i] = words[:, i, :]
+            nc.sync.dma_start(
+                out=words[:].bitcast(I32),
+                in_=w8_words[first : first + count].rearrange("a p n i -> p a (n i)").bitcast(I32),
+            )
 
         def load_w4(first, count):
             words = keep.tile([P, count, 2 * M], U8, align_bytes=64, name="w4_%d" % first)
@@ -70,16 +71,16 @@ def tile_mix_glu48_fm_none_kernel(tc, x, w4_words, w4_scales, w8_words, w8_scale
 
         def load_sc8():
             for q in range(4):
-                nc.scalar.dma_start(
+                nc.sync.dma_start(
                     out=sc8[32 * q : 32 * q + 16, :].bitcast(I32),
                     in_=w8_scales[:, 4 * q : 4 * q + 4, :].bitcast(I32),
                 )
 
         def load_sc4():
-            for q in range(4):
-                nc.scalar.dma_start(
-                    out=sc4[32 * q : 32 * q + 4, :].bitcast(I32).rearrange("r (a n) -> r a n", a=PASSES),
-                    in_=w4_scales[:, 4 * q : 4 * q + 4, :].bitcast(I32).rearrange("a r n -> r a n"),
+            for r in range(4):
+                nc.sync.dma_start(
+                    out=sc4[r:P:32, :].bitcast(I32).rearrange("q (a n) -> q a n", a=PASSES),
+                    in_=w4_scales[:, r:16:4, :].bitcast(I32).rearrange("a q n -> q a n"),
                 )
 
         grouped = {}
@@ -110,23 +111,6 @@ def tile_mix_glu48_fm_none_kernel(tc, x, w4_words, w4_scales, w8_words, w8_scale
                 scales=scales[h, a][:, lo:hi],
                 in_=grouped[h, a][:, lo:hi, :].rearrange("p w j -> p (w j)"),
             )
-
-        def side_shared(h, a, side, v_cols=V_OF_SIDE):
-            lo = SIDE * side
-            copy_v(h, a, lo, lo + v_cols)
-            copy_s(h, a, lo + v_cols, lo + SIDE)
-            quantize(h, a, lo, lo + SIDE)
-
-        def side_on_vector(h, a, side):
-            copy_v(h, a, SIDE * side, SIDE * (side + 1))
-            quantize(h, a, SIDE * side, SIDE * (side + 1))
-
-        def chunk_shared(h, a):
-            copy_v(h, a, 0, SIDE)
-            copy_v(h, a, SIDE, V_OF_HALF)
-            copy_s(h, a, V_OF_HALF, HALF)
-            quantize(h, a, 0, SIDE)
-            quantize(h, a, SIDE, HALF)
 
         banks = {}
         filled = {}
@@ -168,17 +152,21 @@ def tile_mix_glu48_fm_none_kernel(tc, x, w4_words, w4_scales, w8_words, w8_scale
             for m in range(ROW_TILES):
                 pass_g(h, a, m)
 
-        def passes_u(h, a):
+        def passes_u(h, a, lo=0, hi=HALF):
             for m in range(ROW_TILES):
-                pass_u(h, a, m)
+                pass_u(h, a, m, lo, hi)
 
         def shared_g(a, side):
-            for lo in range(SIDE * side, SIDE * (side + 1), NARROW):
-                for m in SHARED:
+            for m in SHARED:
+                for lo in range(SIDE * side, SIDE * (side + 1), NARROW):
                     pass_g(1, a, m, lo, lo + NARROW)
 
-        def shared_u(a, side):
-            for m in SHARED:
+        def own_g(a):
+            for m in OWN:
+                pass_g(1, a, m)
+
+        def side_u(a, side, tiles):
+            for m in tiles:
                 pass_u(1, a, m, SIDE * side, SIDE * (side + 1))
 
         gate = {}
@@ -198,101 +186,96 @@ def tile_mix_glu48_fm_none_kernel(tc, x, w4_words, w4_scales, w8_words, w8_scale
                 out=res[h, m][:, lo:hi], in0=sums("u", h, m, lo, hi), in1=gate[h, m][:, lo:hi], op=ALU.mult
             )
 
-        def finish(m, side):
-            lo, hi = SIDE * side, SIDE * (side + 1)
-            silu(1, m, lo, hi)
-            product(1, m, lo, hi)
+        def store(m, lo, hi):
             nc.sync.dma_start(out=out[P * m : P * (m + 1), HALF + lo : HALF + hi], in_=res[1, m][:, lo:hi])
+
+        def side_shared(h, a, side, v_cols):
+            lo = SIDE * side
+            copy_v(h, a, lo, lo + v_cols)
+            copy_s(h, a, lo + v_cols, lo + SIDE)
+            quantize(h, a, lo, lo + SIDE)
+
+        def chunk_shared(h, a, v_cols=320):
+            copy_v(h, a, 0, SIDE)
+            copy_v(h, a, SIDE, v_cols)
+            copy_s(h, a, v_cols, HALF)
+            quantize(h, a, 0, SIDE)
+            quantize(h, a, SIDE, HALF)
 
         whole = (0, HALF)
         sides = (0, SIDE, HALF)
-        load_sc8()
-        load_x(0, 0, sides)
-        load_w8(0)
-        load_x(0, 1, whole)
+        warm = keep.tile([P, 1], F32, name="warm")
+        nc.scalar.activation(out=warm[:], in_=sc8[:, 0:4].bitcast(F32), func=ACT.Silu)
+
+        load_x(0, 0, whole)
         load_sc4()
-        load_w4(0, 2)
-        load_w8(1)
+        load_w4(0, PASSES)
+        load_x(0, 1, whole)
+        load_w8(0, 2)
+        load_sc8()
         load_x(0, 2, whole)
-        load_w8(2)
-        load_w4(2, 1)
-        load_x(0, LAST, sides)
-        load_w4(LAST, 1)
+        load_w8(2, 1)
+        load_x(0, LAST, whole)
         load_x(1, 0, sides)
-        load_w8(LAST)
+        load_w8(LAST, 1)
         load_x(1, 1, sides)
         load_x(1, 2, sides)
-        load_x(1, LAST, (0, SIDE, SIDE + NARROW, HALF))
+        load_x(1, LAST, sides)
 
-        side_on_vector(0, 0, 0)
-        side_on_vector(0, 0, 1)
-        passes_u(0, 0)
-        passes_g(0, 0)
-        for a in range(1, LAST):
-            chunk_shared(0, a)
-            passes_u(0, a)
+        for a in range(PASSES):
+            chunk_shared(0, a, 320)
             passes_g(0, a)
-        side_shared(0, LAST, 0)
-        side_on_vector(0, LAST, 1)
-        passes_g(0, LAST)
+            if a == 1:
+                passes_u(0, 0)
+            if 0 < a < LAST:
+                passes_u(0, a)
+        copy_s(1, 0, 160, SIDE)
+        copy_v(1, 0, 0, 160)
         passes_u(0, LAST)
-
         for m in range(ROW_TILES):
             silu(0, m)
-        side_on_vector(1, 0, 0)
-        side_on_vector(1, 0, 1)
-        for m in OWN:
-            pass_g(1, 0, m)
+        copy_v(1, 0, SIDE, HALF)
+        quantize(1, 0, 0, SIDE)
+        quantize(1, 0, SIDE, HALF)
+        own_g(0)
         shared_g(0, 0)
         shared_g(0, 1)
         for m in OWN:
             product(0, m)
             pass_u(1, 0, m)
-
-        side_shared(1, 1, 0, V_BETWEEN_PRODUCTS)
-        shared_g(1, 0)
-        for m in OWN:
-            pass_u(1, 1, m, 0, SIDE)
-        copy_s(1, 1, SIDE, HALF)
-        product(0, SHARED[0])
-        shared_u(0, 0)
-        shared_u(1, 0)
-        product(0, SHARED[1])
-        shared_u(0, 1)
+        for side in range(2):
+            product(0, SHARED[side])
+            side_u(0, side, SHARED)
+        copy_s(1, 1, 0, SIDE)
+        copy_s(1, 1, SIDE, SIDE + 128)
+        quantize(1, 1, 0, SIDE)
+        copy_v(1, 1, SIDE + 128, HALF)
         quantize(1, 1, SIDE, HALF)
-        for m in OWN:
-            pass_g(1, 1, m)
-            pass_u(1, 1, m, SIDE, HALF)
-        shared_g(1, 1)
-        shared_u(1, 1)
-
-        side_shared(1, 2, 0, V_AFTER_PRODUCTS)
-        shared_g(2, 0)
-        shared_u(2, 0)
-        side_shared(1, 2, 1)
-        for m in OWN:
-            pass_g(1, 2, m)
-        shared_g(2, 1)
-
-        side_shared(1, LAST, 0)
+        for a in (1, 2):
+            if a == 2:
+                side_shared(1, 2, 0, 160)
+                side_shared(1, 2, 1, 160)
+            shared_g(a, 0)
+            side_u(a, 0, SHARED)
+            side_u(1, a - 1, OWN)
+            own_g(a)
+            shared_g(a, 1)
+            side_u(a, 1, SHARED)
+        side_shared(1, LAST, 0, 160)
+        side_shared(1, LAST, 1, 160)
         shared_g(LAST, 0)
-        shared_u(LAST, 0)
-        shared_u(2, 1)
-        copy_s(1, LAST, SIDE, SIDE + NARROW)
-        copy_v(1, LAST, SIDE + NARROW, HALF)
-        quantize(1, LAST, SIDE, SIDE + NARROW)
-        quantize(1, LAST, SIDE + NARROW, HALF)
+        side_u(LAST, 0, SHARED)
+        pass_u(1, 2, OWN[0])
         shared_g(LAST, 1)
-        shared_u(LAST, 1)
-        for m in OWN:
-            pass_g(1, LAST, m)
-            pass_u(1, 2, m)
-            pass_u(1, LAST, m)
+        side_u(LAST, 1, SHARED)
+        pass_g(1, LAST, 0)
+        pass_u(1, LAST, 0)
+        pass_g(1, LAST, 1)
+        pass_u(1, 2, OWN[1])
+        pass_u(1, LAST, 1)
 
         nc.sync.dma_start(out=out[:, 0:HALF].rearrange("(m p) w -> p m w", p=P), in_=first_half[:])
-        for side in range(2):
-            for m in SHARED:
-                finish(m, side)
-        for m in OWN:
-            for side in range(2):
-                finish(m, side)
+        for m, side in [(m, side) for side in range(2) for m in SHARED] + [(m, side) for m in OWN for side in range(2)]:
+            silu(1, m, SIDE * side, SIDE * (side + 1))
+            product(1, m, SIDE * side, SIDE * (side + 1))
+            store(m, SIDE * side, SIDE * (side + 1))

@@ -34,9 +34,9 @@ def tile_mix_glu48_fm_none_kernel(tc, x, w4_words, w4_scales, w8_words, w8_scale
         ctx.enter_context(tc.manual_schedule())
 
         sc4 = keep.tile([P, PASSES * M], U8, align_bytes=64, name="sc4")
-        sc8 = keep.tile([P, M], U8, align_bytes=64, name="sc8")
-        nc.vector.memset(sc4[:].bitcast(I32), 0)
+        sc8 = keep.tile([P, M + 64], U8, align_bytes=64, name="sc8")
         nc.vector.memset(sc8[:].bitcast(I32), 0)
+        nc.vector.memset(sc4[:].bitcast(I32), 0)
 
         raw = {}
         w4 = {}
@@ -71,8 +71,8 @@ def tile_mix_glu48_fm_none_kernel(tc, x, w4_words, w4_scales, w8_words, w8_scale
 
         def load_sc8():
             for q in range(4):
-                nc.sync.dma_start(
-                    out=sc8[32 * q : 32 * q + 16, :].bitcast(I32),
+                nc.gpsimd.dma_start(
+                    out=sc8[32 * q : 32 * q + 16, 0:M].bitcast(I32),
                     in_=w8_scales[:, 4 * q : 4 * q + 4, :].bitcast(I32),
                 )
 
@@ -157,8 +157,8 @@ def tile_mix_glu48_fm_none_kernel(tc, x, w4_words, w4_scales, w8_words, w8_scale
                 pass_u(h, a, m, lo, hi)
 
         def shared_g(a, side):
-            for m in SHARED:
-                for lo in range(SIDE * side, SIDE * (side + 1), NARROW):
+            for lo in range(SIDE * side, SIDE * (side + 1), NARROW):
+                for m in SHARED:
                     pass_g(1, a, m, lo, lo + NARROW)
 
         def own_g(a):
@@ -205,14 +205,14 @@ def tile_mix_glu48_fm_none_kernel(tc, x, w4_words, w4_scales, w8_words, w8_scale
         whole = (0, HALF)
         sides = (0, SIDE, HALF)
         warm = keep.tile([P, 1], F32, name="warm")
-        nc.scalar.activation(out=warm[:], in_=sc8[:, 0:4].bitcast(F32), func=ACT.Silu)
+        nc.scalar.activation(out=warm[:], in_=sc8[:, M : M + 4].bitcast(F32), func=ACT.Silu)
 
+        load_sc8()
         load_x(0, 0, whole)
         load_sc4()
         load_w4(0, PASSES)
         load_x(0, 1, whole)
         load_w8(0, 2)
-        load_sc8()
         load_x(0, 2, whole)
         load_w8(2, 1)
         load_x(0, LAST, whole)
@@ -262,13 +262,18 @@ def tile_mix_glu48_fm_none_kernel(tc, x, w4_words, w4_scales, w8_words, w8_scale
             shared_g(a, 1)
             side_u(a, 1, SHARED)
         side_shared(1, LAST, 0, 160)
-        side_shared(1, LAST, 1, 160)
+        copy_v(1, LAST, SIDE, SIDE + NARROW)
+        copy_v(1, LAST, SIDE + NARROW, SIDE + 160)
+        copy_s(1, LAST, SIDE + 160, HALF)
+        quantize(1, LAST, SIDE, SIDE + NARROW)
+        quantize(1, LAST, SIDE + NARROW, HALF)
         shared_g(LAST, 0)
         side_u(LAST, 0, SHARED)
-        pass_u(1, 2, OWN[0])
+        pass_u(1, 2, OWN[0], 0, SIDE)
         shared_g(LAST, 1)
         side_u(LAST, 1, SHARED)
         pass_g(1, LAST, 0)
+        pass_u(1, 2, OWN[0], SIDE, HALF)
         pass_u(1, LAST, 0)
         pass_g(1, LAST, 1)
         pass_u(1, 2, OWN[1])

@@ -33,8 +33,8 @@ def tile_mix_glu48_fm_none_kernel(tc, x, w4_words, w4_scales, w8_words, w8_scale
         psum = ctx.enter_context(tc.psum_pool(name="psum", bufs=1))
         ctx.enter_context(tc.manual_schedule())
 
-        sc4 = keep.tile([P, PASSES * M], U8, align_bytes=64, name="sc4")
-        sc8 = keep.tile([P, M + 64], U8, align_bytes=64, name="sc8")
+        sc4 = keep.tile([P, PASSES * M], U8, align_bytes=256, name="sc4")
+        sc8 = keep.tile([P, M + 64], U8, align_bytes=256, name="sc8")
         nc.vector.memset(sc8[:].bitcast(I32), 0)
         nc.vector.memset(sc4[:].bitcast(I32), 0)
 
@@ -44,7 +44,7 @@ def tile_mix_glu48_fm_none_kernel(tc, x, w4_words, w4_scales, w8_words, w8_scale
 
         def load_x(h, a, cuts):
             for lo, hi in zip(cuts, cuts[1:]):
-                piece = keep.tile([P, 4, hi - lo], F32, align_bytes=64, name="raw_%d_%d_%d" % (h, a, lo))
+                piece = keep.tile([P, 4, hi - lo], F32, align_bytes=256, name="raw_%d_%d_%d" % (h, a, lo))
                 raw.setdefault((h, a), []).append((lo, hi, piece))
                 nc.sync.dma_start(
                     out=piece[:],
@@ -52,7 +52,7 @@ def tile_mix_glu48_fm_none_kernel(tc, x, w4_words, w4_scales, w8_words, w8_scale
                 )
 
         def load_w8(first, count):
-            words = keep.tile([P, count, 4 * M], U8, align_bytes=64, name="w8_%d" % first)
+            words = keep.tile([P, count, 4 * M], U8, align_bytes=256, name="w8_%d" % first)
             for i in range(count):
                 w8[first + i] = words[:, i, :]
             nc.sync.dma_start(
@@ -61,7 +61,7 @@ def tile_mix_glu48_fm_none_kernel(tc, x, w4_words, w4_scales, w8_words, w8_scale
             )
 
         def load_w4(first, count):
-            words = keep.tile([P, count, 2 * M], U8, align_bytes=64, name="w4_%d" % first)
+            words = keep.tile([P, count, 2 * M], U8, align_bytes=256, name="w4_%d" % first)
             for i in range(count):
                 w4[first + i] = words[:, i, :]
             nc.sync.dma_start(
@@ -88,9 +88,9 @@ def tile_mix_glu48_fm_none_kernel(tc, x, w4_words, w4_scales, w8_words, w8_scale
         scales = {}
         for h in range(2):
             for a in range(PASSES):
-                grouped[h, a] = keep.tile([P, HALF, 4], BF16, align_bytes=64, name="grouped_%d_%d" % (h, a))
-                codes[h, a] = keep.tile([P, HALF], U32, align_bytes=64, name="codes_%d_%d" % (h, a))
-                scales[h, a] = keep.tile([P, HALF], U8, align_bytes=64, name="scales_%d_%d" % (h, a))
+                grouped[h, a] = keep.tile([P, HALF, 4], BF16, align_bytes=256, name="grouped_%d_%d" % (h, a))
+                codes[h, a] = keep.tile([P, HALF], U32, align_bytes=256, name="codes_%d_%d" % (h, a))
+                scales[h, a] = keep.tile([P, HALF], U8, align_bytes=256, name="scales_%d_%d" % (h, a))
 
         def interleave(engine_copy, h, a, lo, hi):
             base, piece = [(begin, tile) for begin, end, tile in raw[h, a] if begin <= lo and hi <= end][0]
@@ -171,12 +171,12 @@ def tile_mix_glu48_fm_none_kernel(tc, x, w4_words, w4_scales, w8_words, w8_scale
 
         gate = {}
         res = {}
-        first_half = keep.tile([P, ROW_TILES, HALF], F32, align_bytes=64, name="first_half")
+        first_half = keep.tile([P, ROW_TILES, HALF], F32, align_bytes=256, name="first_half")
         for m in range(ROW_TILES):
             res[0, m] = first_half[:, m, :]
-            res[1, m] = keep.tile([P, HALF], F32, align_bytes=64, name="res_%d" % m)
+            res[1, m] = keep.tile([P, HALF], F32, align_bytes=256, name="res_%d" % m)
             for h in range(2):
-                gate[h, m] = keep.tile([P, HALF], F32, align_bytes=64, name="gate_%d_%d" % (h, m))
+                gate[h, m] = keep.tile([P, HALF], F32, align_bytes=256, name="gate_%d_%d" % (h, m))
 
         def silu(h, m, lo=0, hi=HALF):
             nc.scalar.activation(out=gate[h, m][:, lo:hi], in_=sums("g", h, m, lo, hi), func=ACT.Silu)

@@ -207,80 +207,118 @@ def tile_mix_glu48_fm_none_kernel(tc, x, w4_words, w4_scales, w8_words, w8_scale
         warm = keep.tile([P, 1], F32, name="warm")
         nc.scalar.activation(out=warm[:], in_=sc8[:, M : M + 4].bitcast(F32), func=ACT.Silu)
 
+        def prep(h, a, v=160):
+            copy_v(h, a, 0, v)
+            copy_s(h, a, v, SIDE)
+            copy_v(h, a, SIDE, SIDE + v)
+            copy_s(h, a, SIDE + v, HALF)
+            quantize(h, a, 0, SIDE)
+            quantize(h, a, SIDE, HALF)
+
+        def cv(a, s, lo, hi):
+            copy_v(1, a, SIDE * s + lo, SIDE * s + hi)
+
+        def cs(a, s, lo, hi):
+            copy_s(1, a, SIDE * s + lo, SIDE * s + hi)
+
+        def qz(a, s):
+            quantize(1, a, SIDE * s, SIDE * (s + 1))
+
+        def fin(m, s):
+            silu(1, m, SIDE * s, SIDE * (s + 1))
+            product(1, m, SIDE * s, SIDE * (s + 1))
+            store(m, SIDE * s, SIDE * (s + 1))
+
         load_sc8()
         load_x(0, 0, whole)
         load_sc4()
         load_w4(0, PASSES)
+        load_w8(0, 1)
         load_x(0, 1, whole)
-        load_w8(0, 2)
+        load_w8(1, 1)
         load_x(0, 2, whole)
+        load_x(0, 3, whole)
         load_w8(2, 1)
-        load_x(0, LAST, whole)
-        load_x(1, 0, sides)
-        load_w8(LAST, 1)
-        load_x(1, 1, sides)
-        load_x(1, 2, sides)
-        load_x(1, LAST, sides)
-
-        for a in range(PASSES):
-            chunk_shared(0, a, 320)
+        load_x(1, 0, (0, 256))
+        load_x(1, 0, (256, 512))
+        load_w8(3, 1)
+        load_x(1, 1, (0, 256))
+        load_x(1, 1, (256, 512))
+        load_x(1, 2, (0, 256))
+        load_x(1, 3, (0, 256))
+        load_x(1, 2, (256, 512))
+        load_x(1, 3, (256, 512))
+        for a in range(3):
+            prep(0, a)
             passes_g(0, a)
-            if a == 1:
-                passes_u(0, 0)
-            if 0 < a < LAST:
+            if a < 2:
                 passes_u(0, a)
-        copy_s(1, 0, 160, SIDE)
-        copy_v(1, 0, 0, 160)
-        passes_u(0, LAST)
-        for m in range(ROW_TILES):
-            silu(0, m)
-        copy_v(1, 0, SIDE, HALF)
-        quantize(1, 0, 0, SIDE)
-        quantize(1, 0, SIDE, HALF)
-        own_g(0)
+        prep(0, 3)
+        passes_u(0, 2)
+        for m in (2, 0, 1, 3):
+            pass_g(0, 3, m)
+        cv(0, 0, 0, 160)
+        cs(0, 0, 160, 256)
+        silu(0, 2)
+        qz(0, 0)
+        silu(0, 0)
+        cv(0, 1, 0, 256)
+        silu(0, 1)
+        silu(0, 3)
+        qz(0, 1)
         shared_g(0, 0)
+        for m in (2, 0, 1, 3):
+            pass_u(0, 3, m)
+        own_g(0)
         shared_g(0, 1)
-        for m in OWN:
-            product(0, m)
-            pass_u(1, 0, m)
-        for side in range(2):
-            product(0, SHARED[side])
-            side_u(0, side, SHARED)
-        copy_s(1, 1, 0, SIDE)
-        copy_s(1, 1, SIDE, SIDE + 128)
-        quantize(1, 1, 0, SIDE)
-        copy_v(1, 1, SIDE + 128, HALF)
-        quantize(1, 1, SIDE, HALF)
-        for a in (1, 2):
-            if a == 2:
-                side_shared(1, 2, 0, 160)
-                side_shared(1, 2, 1, 160)
-            shared_g(a, 0)
-            side_u(a, 0, SHARED)
-            side_u(1, a - 1, OWN)
-            own_g(a)
-            shared_g(a, 1)
-            side_u(a, 1, SHARED)
-        side_shared(1, LAST, 0, 160)
-        copy_v(1, LAST, SIDE, SIDE + NARROW)
-        copy_v(1, LAST, SIDE + NARROW, SIDE + 160)
-        copy_s(1, LAST, SIDE + 160, HALF)
-        quantize(1, LAST, SIDE, SIDE + NARROW)
-        quantize(1, LAST, SIDE + NARROW, HALF)
-        shared_g(LAST, 0)
-        side_u(LAST, 0, SHARED)
-        pass_u(1, 2, OWN[0], 0, SIDE)
-        shared_g(LAST, 1)
-        side_u(LAST, 1, SHARED)
-        pass_g(1, LAST, 0)
-        pass_u(1, 2, OWN[0], SIDE, HALF)
-        pass_u(1, LAST, 0)
-        pass_g(1, LAST, 1)
-        pass_u(1, 2, OWN[1])
-        pass_u(1, LAST, 1)
-
+        product(0, 2)
+        side_u(0, 0, SHARED)
+        product(0, 0)
+        pass_u(1, 0, 0)
+        cs(1, 0, 0, 192)
+        cv(1, 0, 192, 256)
+        product(0, 1)
+        pass_u(1, 0, 1)
+        qz(1, 0)
+        cs(1, 1, 128, 256)
+        cv(1, 1, 0, 128)
+        product(0, 3)
+        qz(1, 1)
+        shared_g(1, 0)
+        side_u(1, 0, SHARED)
+        side_u(1, 0, OWN)
+        side_u(0, 1, SHARED)
+        own_g(1)
+        side_shared(1, 2, 0, 160)
+        shared_g(1, 1)
+        side_u(1, 1, SHARED)
+        shared_g(2, 0)
+        side_u(2, 0, SHARED)
+        side_shared(1, 3, 0, 160)
+        pass_u(1, 1, 0, SIDE, HALF)
+        shared_g(3, 0)
+        side_u(3, 0, SHARED)
+        side_shared(1, 2, 1, 160)
+        pass_u(1, 1, 1, SIDE, HALF)
+        pass_u(1, 2, 0, 0, SIDE)
+        pass_u(1, 3, 0, 0, SIDE)
+        shared_g(2, 1)
+        side_u(2, 1, SHARED)
+        pass_g(1, 2, 0)
+        pass_u(1, 2, 0, SIDE, HALF)
+        cv(3, 1, 0, 128)
+        cv(3, 1, 128, 160)
+        cs(3, 1, 160, 256)
+        quantize(1, 3, SIDE, SIDE + NARROW)
+        quantize(1, 3, SIDE + NARROW, HALF)
+        shared_g(3, 1)
+        side_u(3, 1, SHARED)
+        pass_g(1, 3, 0)
+        pass_u(1, 3, 0, SIDE, HALF)
+        pass_g(1, 2, 1)
+        pass_g(1, 3, 1)
+        pass_u(1, 2, 1)
+        pass_u(1, 3, 1)
         nc.sync.dma_start(out=out[:, 0:HALF].rearrange("(m p) w -> p m w", p=P), in_=first_half[:])
-        for m, side in [(m, side) for side in range(2) for m in SHARED] + [(m, side) for m in OWN for side in range(2)]:
-            silu(1, m, SIDE * side, SIDE * (side + 1))
-            product(1, m, SIDE * side, SIDE * (side + 1))
-            store(m, SIDE * side, SIDE * (side + 1))
+        for m, side in [(2, 0), (3, 0), (2, 1), (3, 1), (0, 0), (0, 1), (1, 0), (1, 1)]:
+            fin(m, side)

@@ -18,12 +18,21 @@ ALU = mybir.AluOpType
 P = 128
 PASSES = K // 512
 LAST = PASSES - 1
-HALF = 512
-SIDE = 256
 ROW_TILES = M // P
-NARROW = 128
-OWN = (0, 1)
-SHARED = (2, 3)
+BANK = 512
+HALF = 512
+STRIP = 256
+ALIGN = 256
+
+
+def place(kind, m, lo):
+    if lo < HALF:
+        return "%s_%d" % (kind, m), "%s_%d" % (kind, m), lo
+    if lo < HALF + STRIP:
+        return "left_%d" % m, "g_%d" % m, (STRIP if kind == "u" else 0) + lo % STRIP
+    if m < 2:
+        return "right_%d" % m, "u_%d" % m, (STRIP if kind == "u" else 0) + lo % STRIP
+    return "right_%s" % kind, "u_%d" % (2 if kind == "g" else 3), STRIP * (m - 2) + lo % STRIP
 
 
 def tile_mix_glu48_fm_none_kernel(tc, x, w4_words, w4_scales, w8_words, w8_scales, out):
@@ -33,8 +42,8 @@ def tile_mix_glu48_fm_none_kernel(tc, x, w4_words, w4_scales, w8_words, w8_scale
         psum = ctx.enter_context(tc.psum_pool(name="psum", bufs=1))
         ctx.enter_context(tc.manual_schedule())
 
-        sc4 = keep.tile([P, PASSES * M], U8, align_bytes=256, name="sc4")
-        sc8 = keep.tile([P, M + 64], U8, align_bytes=256, name="sc8")
+        sc4 = keep.tile([P, PASSES * M], U8, align_bytes=ALIGN, name="sc4")
+        sc8 = keep.tile([P, M + 64], U8, align_bytes=ALIGN, name="sc8")
         nc.vector.memset(sc8[:].bitcast(I32), 0)
         nc.vector.memset(sc4[:].bitcast(I32), 0)
 
@@ -42,17 +51,15 @@ def tile_mix_glu48_fm_none_kernel(tc, x, w4_words, w4_scales, w8_words, w8_scale
         w4 = {}
         w8 = {}
 
-        def load_x(h, a, cuts):
-            for lo, hi in zip(cuts, cuts[1:]):
-                piece = keep.tile([P, 4, hi - lo], F32, align_bytes=256, name="raw_%d_%d_%d" % (h, a, lo))
-                raw.setdefault((h, a), []).append((lo, hi, piece))
-                nc.sync.dma_start(
-                    out=piece[:],
-                    in_=x[512 * a : 512 * (a + 1), HALF * h + lo : HALF * h + hi].rearrange("(p j) w -> p j w", j=4),
-                )
+        def load_x(a, lo, hi):
+            piece = keep.tile([P, 4, hi - lo], F32, align_bytes=ALIGN, name="raw_%d_%d" % (a, lo))
+            raw.setdefault(a, []).append((lo, hi, piece))
+            nc.sync.dma_start(
+                out=piece[:], in_=x[512 * a : 512 * (a + 1), lo:hi].rearrange("(p j) w -> p j w", j=4)
+            )
 
         def load_w8(first, count):
-            words = keep.tile([P, count, 4 * M], U8, align_bytes=256, name="w8_%d" % first)
+            words = keep.tile([P, count, 4 * M], U8, align_bytes=ALIGN, name="w8_%d" % first)
             for i in range(count):
                 w8[first + i] = words[:, i, :]
             nc.sync.dma_start(
@@ -61,7 +68,7 @@ def tile_mix_glu48_fm_none_kernel(tc, x, w4_words, w4_scales, w8_words, w8_scale
             )
 
         def load_w4(first, count):
-            words = keep.tile([P, count, 2 * M], U8, align_bytes=256, name="w4_%d" % first)
+            words = keep.tile([P, count, 2 * M], U8, align_bytes=ALIGN, name="w4_%d" % first)
             for i in range(count):
                 w4[first + i] = words[:, i, :]
             nc.sync.dma_start(
@@ -83,242 +90,196 @@ def tile_mix_glu48_fm_none_kernel(tc, x, w4_words, w4_scales, w8_words, w8_scale
                     in_=w4_scales[:, r:16:4, :].bitcast(I32).rearrange("a q n -> q a n"),
                 )
 
-        grouped = {}
-        codes = {}
-        scales = {}
-        for h in range(2):
-            for a in range(PASSES):
-                grouped[h, a] = keep.tile([P, HALF, 4], BF16, align_bytes=256, name="grouped_%d_%d" % (h, a))
-                codes[h, a] = keep.tile([P, HALF], U32, align_bytes=256, name="codes_%d_%d" % (h, a))
-                scales[h, a] = keep.tile([P, HALF], U8, align_bytes=256, name="scales_%d_%d" % (h, a))
+        grouped = []
+        codes = []
+        scales = []
+        for a in range(PASSES):
+            grouped.append(keep.tile([P, T, 4], BF16, align_bytes=ALIGN, name="grouped_%d" % a))
+            codes.append(keep.tile([P, T], U32, align_bytes=ALIGN, name="codes_%d" % a))
+            scales.append(keep.tile([P, T], U8, align_bytes=ALIGN, name="scales_%d" % a))
 
-        def interleave(engine_copy, h, a, lo, hi):
-            base, piece = [(begin, tile) for begin, end, tile in raw[h, a] if begin <= lo and hi <= end][0]
+        def interleave(engine_copy, a, lo, hi):
+            base, piece = [(begin, tile) for begin, end, tile in raw[a] if begin <= lo and hi <= end][0]
             engine_copy(
-                out=grouped[h, a][:, lo:hi, :].rearrange("p (c i) j -> p c j i", i=4),
+                out=grouped[a][:, lo:hi, :].rearrange("p (c i) j -> p c j i", i=4),
                 in_=piece[:, :, lo - base : hi - base].rearrange("p j (c i) -> p c j i", i=4),
             )
 
-        def copy_v(h, a, lo, hi):
-            interleave(nc.vector.tensor_copy, h, a, lo, hi)
+        def copy_v(a, lo, hi):
+            interleave(nc.vector.tensor_copy, a, lo, hi)
 
-        def copy_s(h, a, lo, hi):
-            interleave(nc.scalar.copy, h, a, lo, hi)
+        def copy_s(a, lo, hi):
+            interleave(nc.scalar.copy, a, lo, hi)
 
-        def quantize(h, a, lo, hi):
+        def quantize(a, lo, hi):
             nc.vector.quantize_mx(
-                out=codes[h, a][:, lo:hi].bitcast(FP8X4),
-                scales=scales[h, a][:, lo:hi],
-                in_=grouped[h, a][:, lo:hi, :].rearrange("p w j -> p (w j)"),
+                out=codes[a][:, lo:hi].bitcast(FP8X4),
+                scales=scales[a][:, lo:hi],
+                in_=grouped[a][:, lo:hi, :].rearrange("p w j -> p (w j)"),
             )
 
         banks = {}
         filled = {}
 
-        def place(h, m, lo):
-            if h == 1 and m in SHARED:
-                return SHARED[lo // SIDE], SIDE * SHARED.index(m) + lo % SIDE
-            return m, lo
+        def sums(kind, m, lo, hi):
+            key, tag, at = place(kind, m, lo)
+            return banks[key][:, at : at + hi - lo]
 
-        def sums(kind, h, m, lo, hi):
-            bank, at = place(h, m, lo)
-            return banks[kind, h, bank][:, at : at + hi - lo]
-
-        def multiply(kind, h, a, m, lo, hi, words, word_scales):
-            key = (kind, h, place(h, m, lo)[0])
+        def multiply(kind, a, m, lo, hi):
+            key, tag, at = place(kind, m, lo)
             if key not in banks:
-                banks[key] = psum.tile([P, HALF], F32, name="%s_%d_%d" % key, tag="%s_%d" % (kind, key[2]))
+                banks[key] = psum.tile([P, BANK], F32, name=key, tag=tag)
             before = filled.get(key, 0)
             filled[key] = before + hi - lo
+            if kind == "g":
+                words = w4[a][:, 2 * P * m : 2 * P * (m + 1)].bitcast(FP4X4)
+                word_scales = sc4[:, M * a + P * m : M * a + P * (m + 1)]
+            else:
+                words = w8[a][:, 4 * P * m : 4 * P * (m + 1)].bitcast(FP8X4)
+                word_scales = sc8[4 * a : P, P * m : P * (m + 1)]
             nc.tensor.matmul_mx(
-                out=sums(kind, h, m, lo, hi),
+                out=sums(kind, m, lo, hi),
                 lhsT=words,
                 lhsT_scale=word_scales,
-                rhs=codes[h, a][:, lo:hi].bitcast(FP8X4),
-                rhs_scale=scales[h, a][:, lo:hi],
+                rhs=codes[a][:, lo:hi].bitcast(FP8X4),
+                rhs_scale=scales[a][:, lo:hi],
                 start=(before == 0),
-                stop=(filled[key] == PASSES * HALF),
+                stop=(filled[key] == PASSES * BANK),
             )
 
-        def pass_g(h, a, m, lo=0, hi=HALF):
-            words = w4[a][:, 2 * P * m : 2 * P * (m + 1)].bitcast(FP4X4)
-            multiply("g", h, a, m, lo, hi, words, sc4[:, M * a + P * m : M * a + P * (m + 1)])
-
-        def pass_u(h, a, m, lo=0, hi=HALF):
-            words = w8[a][:, 4 * P * m : 4 * P * (m + 1)].bitcast(FP8X4)
-            multiply("u", h, a, m, lo, hi, words, sc8[4 * a : P, P * m : P * (m + 1)])
-
-        def passes_g(h, a):
-            for m in range(ROW_TILES):
-                pass_g(h, a, m)
-
-        def passes_u(h, a, lo=0, hi=HALF):
-            for m in range(ROW_TILES):
-                pass_u(h, a, m, lo, hi)
-
-        def shared_g(a, side):
-            for lo in range(SIDE * side, SIDE * (side + 1), NARROW):
-                for m in SHARED:
-                    pass_g(1, a, m, lo, lo + NARROW)
-
-        def own_g(a):
-            for m in OWN:
-                pass_g(1, a, m)
-
-        def side_u(a, side, tiles):
-            for m in tiles:
-                pass_u(1, a, m, SIDE * side, SIDE * (side + 1))
-
-        gate = {}
+        gate = keep.tile([P, ROW_TILES * T], F32, align_bytes=ALIGN, name="gate")
         res = {}
-        first_half = keep.tile([P, ROW_TILES, HALF], F32, align_bytes=256, name="first_half")
-        for m in range(ROW_TILES):
-            res[0, m] = first_half[:, m, :]
-            res[1, m] = keep.tile([P, HALF], F32, align_bytes=256, name="res_%d" % m)
-            for h in range(2):
-                gate[h, m] = keep.tile([P, HALF], F32, align_bytes=256, name="gate_%d_%d" % (h, m))
 
-        def silu(h, m, lo=0, hi=HALF):
-            nc.scalar.activation(out=gate[h, m][:, lo:hi], in_=sums("g", h, m, lo, hi), func=ACT.Silu)
+        def result_tile(rows, lo, hi):
+            tile = keep.tile([P, len(rows), hi - lo], F32, align_bytes=ALIGN, name="res_%d_%d" % (rows[0], lo))
+            for i, m in enumerate(rows):
+                res.setdefault(m, []).append((lo, hi, tile[:, i, :]))
+            return rows, lo, hi, tile
 
-        def product(h, m, lo=0, hi=HALF):
+        def silu(m, lo, hi):
+            nc.scalar.activation(out=gate[:, T * m + lo : T * m + hi], in_=sums("g", m, lo, hi), func=ACT.Silu)
+
+        def product(m, lo, hi):
+            base, row = [(begin, tile) for begin, end, tile in res[m] if begin <= lo and hi <= end][0]
             nc.vector.tensor_tensor(
-                out=res[h, m][:, lo:hi], in0=sums("u", h, m, lo, hi), in1=gate[h, m][:, lo:hi], op=ALU.mult
+                out=row[:, lo - base : hi - base],
+                in0=sums("u", m, lo, hi),
+                in1=gate[:, T * m + lo : T * m + hi],
+                op=ALU.mult,
             )
 
-        def store(m, lo, hi):
-            nc.sync.dma_start(out=out[P * m : P * (m + 1), HALF + lo : HALF + hi], in_=res[1, m][:, lo:hi])
+        def store(rows, lo, hi, tile):
+            nc.sync.dma_start(
+                out=out[P * rows[0] : P * (rows[-1] + 1), lo:hi].rearrange("(m p) w -> p m w", p=P), in_=tile[:]
+            )
 
-        def side_shared(h, a, side, v_cols):
-            lo = SIDE * side
-            copy_v(h, a, lo, lo + v_cols)
-            copy_s(h, a, lo + v_cols, lo + SIDE)
-            quantize(h, a, lo, lo + SIDE)
-
-        def chunk_shared(h, a, v_cols=320):
-            copy_v(h, a, 0, SIDE)
-            copy_v(h, a, SIDE, v_cols)
-            copy_s(h, a, v_cols, HALF)
-            quantize(h, a, 0, SIDE)
-            quantize(h, a, SIDE, HALF)
-
-        whole = (0, HALF)
-        sides = (0, SIDE, HALF)
         warm = keep.tile([P, 1], F32, name="warm")
         nc.scalar.activation(out=warm[:], in_=sc8[:, M : M + 4].bitcast(F32), func=ACT.Silu)
 
-        def prep(h, a, v=160):
-            copy_v(h, a, 0, v)
-            copy_s(h, a, v, SIDE)
-            copy_v(h, a, SIDE, SIDE + v)
-            copy_s(h, a, SIDE + v, HALF)
-            quantize(h, a, 0, SIDE)
-            quantize(h, a, SIDE, HALF)
-
-        def cv(a, s, lo, hi):
-            copy_v(1, a, SIDE * s + lo, SIDE * s + hi)
-
-        def cs(a, s, lo, hi):
-            copy_s(1, a, SIDE * s + lo, SIDE * s + hi)
-
-        def qz(a, s):
-            quantize(1, a, SIDE * s, SIDE * (s + 1))
-
-        def fin(m, s):
-            silu(1, m, SIDE * s, SIDE * (s + 1))
-            product(1, m, SIDE * s, SIDE * (s + 1))
-            store(m, SIDE * s, SIDE * (s + 1))
+        rows = list(range(ROW_TILES))
+        left, right = HALF, HALF + STRIP
+        first_store = result_tile(rows, 0, HALF)
+        left_stores = [result_tile(pair, left, right) for pair in (rows[:2], rows[2:])]
+        last_stores = [result_tile([m], right, T) for m in rows]
 
         load_sc8()
-        load_x(0, 0, whole)
+        load_x(0, 0, HALF)
         load_sc4()
         load_w4(0, PASSES)
         load_w8(0, 1)
-        load_x(0, 1, whole)
+        load_x(1, 0, HALF)
         load_w8(1, 1)
-        load_x(0, 2, whole)
-        load_x(0, 3, whole)
+        load_x(2, 0, HALF)
+        load_x(3, 0, HALF)
         load_w8(2, 1)
-        load_x(1, 0, (0, 256))
-        load_x(1, 0, (256, 512))
+        load_x(0, left, right)
         load_w8(3, 1)
-        load_x(1, 1, (0, 256))
-        load_x(1, 1, (256, 512))
-        load_x(1, 2, (0, 256))
-        load_x(1, 3, (0, 256))
-        load_x(1, 2, (256, 512))
-        load_x(1, 3, (256, 512))
-        for a in range(3):
-            prep(0, a)
-            passes_g(0, a)
+        for a in range(1, PASSES):
+            load_x(a, left, right)
+        for a in range(PASSES):
+            load_x(a, right, T)
+
+        def copies(a, lo, share):
+            if share > 0:
+                copy_v(a, lo, lo + share)
+            if share < STRIP:
+                copy_s(a, lo + share, lo + STRIP)
+
+        def prepare(a, base, shares):
+            for lo, share in zip((base, base + STRIP), shares):
+                copies(a, lo, share)
+            for lo in (base, base + STRIP):
+                quantize(a, lo, lo + STRIP)
+
+        def whole(kind, a, tiles):
+            for m in tiles:
+                multiply(kind, a, m, 0, HALF)
+
+        def strip(a, lo, tiles, kinds="gu"):
+            for m in tiles:
+                for kind in kinds:
+                    multiply(kind, a, m, lo, lo + STRIP)
+
+        for a in range(LAST):
+            prepare(a, 0, (160, 160))
+            whole("g", a, rows)
             if a < 2:
-                passes_u(0, a)
-        prep(0, 3)
-        passes_u(0, 2)
-        for m in (2, 0, 1, 3):
-            pass_g(0, 3, m)
-        cv(0, 0, 0, 160)
-        cs(0, 0, 160, 256)
-        silu(0, 2)
-        qz(0, 0)
-        silu(0, 0)
-        cv(0, 1, 0, 256)
-        silu(0, 1)
-        silu(0, 3)
-        qz(0, 1)
-        shared_g(0, 0)
-        for m in (2, 0, 1, 3):
-            pass_u(0, 3, m)
-        own_g(0)
-        shared_g(0, 1)
-        product(0, 2)
-        side_u(0, 0, SHARED)
-        product(0, 0)
-        pass_u(1, 0, 0)
-        cs(1, 0, 0, 192)
-        cv(1, 0, 192, 256)
-        product(0, 1)
-        pass_u(1, 0, 1)
-        qz(1, 0)
-        cs(1, 1, 128, 256)
-        cv(1, 1, 0, 128)
-        product(0, 3)
-        qz(1, 1)
-        shared_g(1, 0)
-        side_u(1, 0, SHARED)
-        side_u(1, 0, OWN)
-        side_u(0, 1, SHARED)
-        own_g(1)
-        side_shared(1, 2, 0, 160)
-        shared_g(1, 1)
-        side_u(1, 1, SHARED)
-        shared_g(2, 0)
-        side_u(2, 0, SHARED)
-        side_shared(1, 3, 0, 160)
-        pass_u(1, 1, 0, SIDE, HALF)
-        shared_g(3, 0)
-        side_u(3, 0, SHARED)
-        side_shared(1, 2, 1, 160)
-        pass_u(1, 1, 1, SIDE, HALF)
-        pass_u(1, 2, 0, 0, SIDE)
-        pass_u(1, 3, 0, 0, SIDE)
-        shared_g(2, 1)
-        side_u(2, 1, SHARED)
-        pass_g(1, 2, 0)
-        pass_u(1, 2, 0, SIDE, HALF)
-        cv(3, 1, 0, 128)
-        cv(3, 1, 128, 160)
-        cs(3, 1, 160, 256)
-        quantize(1, 3, SIDE, SIDE + NARROW)
-        quantize(1, 3, SIDE + NARROW, HALF)
-        shared_g(3, 1)
-        side_u(3, 1, SHARED)
-        pass_g(1, 3, 0)
-        pass_u(1, 3, 0, SIDE, HALF)
-        pass_g(1, 2, 1)
-        pass_g(1, 3, 1)
-        pass_u(1, 2, 1)
-        pass_u(1, 3, 1)
-        nc.sync.dma_start(out=out[:, 0:HALF].rearrange("(m p) w -> p m w", p=P), in_=first_half[:])
-        for m, side in [(2, 0), (3, 0), (2, 1), (3, 1), (0, 0), (0, 1), (1, 0), (1, 1)]:
-            fin(m, side)
+                whole("u", a, rows)
+        prepare(LAST, 0, (160, 160))
+        whole("u", 2, rows[:3])
+        for lo in (0, STRIP):
+            for m in rows[:3]:
+                multiply("g", LAST, m, lo, lo + STRIP)
+        whole("g", LAST, rows[3:])
+        whole("u", 2, rows[3:])
+        whole("u", LAST, rows)
+        copies(0, left, 160)
+        quantize(0, left, right)
+        for m in rows:
+            silu(m, 0, HALF)
+        strip(0, left, rows)
+        for at in (left, left + P):
+            copy_v(1, at, at + P)
+        for at in (left, left + P):
+            quantize(1, at, at + P)
+        product(0, 0, HALF)
+        strip(1, left, rows)
+        for a in (2, 3):
+            copies(a, left, 96)
+            product(a - 1, 0, HALF)
+            quantize(a, left, right)
+            strip(a, left, rows)
+        copies(0, right, 96)
+        product(3, 0, HALF)
+        quantize(0, right, T)
+        strip(0, right, [0, 1])
+        strip(0, right, [2, 3], "g")
+        strip(0, right, [2, 3], "u")
+        for a in (1, 2):
+            copies(a, right, 160)
+            if a == 2:
+                product(0, left, right)
+            quantize(a, right, T)
+            strip(a, right, [0, 1])
+            strip(a, right, [2, 3], "g")
+            for m in (2 * a - 2, 2 * a - 1):
+                silu(m, left, right)
+        strip(1, right, [2, 3], "u")
+        copy_v(LAST, right, right + P)
+        copy_v(LAST, right + P, right + 160)
+        copy_s(LAST, right + 160, T)
+        quantize(LAST, right, right + P)
+        quantize(LAST, right + P, T)
+        for m in rows[1:]:
+            product(m, left, right)
+        store(*first_store)
+        for tile in left_stores:
+            store(*tile)
+        strip(LAST, right, [0, 1])
+        strip(LAST, right, [2, 3], "g")
+        for a in (2, 3):
+            strip(a, right, [2, 3], "u")
+        for m in rows:
+            silu(m, right, T)
+            product(m, right, T)
+            store(*last_stores[m])

@@ -22,7 +22,7 @@ ROW_TILES = M // P
 BANK = 512
 HALF = 512
 STRIP = 256
-ALIGN = 256
+ALIGN = 1024
 
 
 def place(kind, m, lo):

from contextlib import ExitStack

import concourse.mybir as mybir

K, M, T = 2048, 512, 1024
FLOPS = 2 * 2 * K * M * T

F32 = mybir.dt.float32
BF16 = mybir.dt.bfloat16
I32 = mybir.dt.int32
U32 = mybir.dt.uint32
U8 = mybir.dt.uint8
FP8X4 = mybir.dt.float8_e4m3fn_x4
FP4X4 = mybir.dt.float4_e2m1fn_x4
ACT = mybir.ActivationFunctionType
ALU = mybir.AluOpType

P = 128
PASSES = K // 512
LAST = PASSES - 1
ROW_TILES = M // P
BANK = 512
HALF = 512
STRIP = 256
ALIGN = 1024


def place(kind, m, lo):
    if lo < HALF:
        return "%s_%d" % (kind, m), "%s_%d" % (kind, m), lo
    if lo < HALF + STRIP:
        return "left_%d" % m, "g_%d" % m, (STRIP if kind == "u" else 0) + lo % STRIP
    if m < 2:
        return "right_%d" % m, "u_%d" % m, (STRIP if kind == "u" else 0) + lo % STRIP
    return "right_%s" % kind, "u_%d" % (2 if kind == "g" else 3), STRIP * (m - 2) + lo % STRIP


def tile_mix_glu48_fm_none_kernel(tc, x, w4_words, w4_scales, w8_words, w8_scales, out):
    nc = tc.nc
    with ExitStack() as ctx:
        keep = ctx.enter_context(tc.tile_pool(name="keep", bufs=1))
        psum = ctx.enter_context(tc.psum_pool(name="psum", bufs=1))
        ctx.enter_context(tc.manual_schedule())

        sc4 = keep.tile([P, PASSES * M], U8, align_bytes=ALIGN, name="sc4")
        sc8 = keep.tile([P, M + 64], U8, align_bytes=ALIGN, name="sc8")
        nc.vector.memset(sc8[:].bitcast(I32), 0)
        nc.vector.memset(sc4[:].bitcast(I32), 0)

        raw = {}
        w4 = {}
        w8 = {}

        def load_x(a, lo, hi):
            piece = keep.tile([P, 4, hi - lo], F32, align_bytes=ALIGN, name="raw_%d_%d" % (a, lo))
            raw.setdefault(a, []).append((lo, hi, piece))
            nc.sync.dma_start(
                out=piece[:], in_=x[512 * a : 512 * (a + 1), lo:hi].rearrange("(p j) w -> p j w", j=4)
            )

        def load_w8(first, count):
            words = keep.tile([P, count, 4 * M], U8, align_bytes=ALIGN, name="w8_%d" % first)
            for i in range(count):
                w8[first + i] = words[:, i, :]
            nc.sync.dma_start(
                out=words[:].bitcast(I32),
                in_=w8_words[first : first + count].rearrange("a p n i -> p a (n i)").bitcast(I32),
            )

        def load_w4(first, count):
            words = keep.tile([P, count, 2 * M], U8, align_bytes=ALIGN, name="w4_%d" % first)
            for i in range(count):
                w4[first + i] = words[:, i, :]
            nc.sync.dma_start(
                out=words[:].bitcast(I32),
                in_=w4_words[first : first + count].rearrange("a p b -> p a b").bitcast(I32),
            )

        def load_sc8():
            for q in range(4):
                nc.gpsimd.dma_start(
                    out=sc8[32 * q : 32 * q + 16, 0:M].bitcast(I32),
                    in_=w8_scales[:, 4 * q : 4 * q + 4, :].bitcast(I32),
                )

        def load_sc4():
            for r in range(4):
                nc.sync.dma_start(
                    out=sc4[r:P:32, :].bitcast(I32).rearrange("q (a n) -> q a n", a=PASSES),
                    in_=w4_scales[:, r:16:4, :].bitcast(I32).rearrange("a q n -> q a n"),
                )

        grouped = []
        codes = []
        scales = []
        for a in range(PASSES):
            grouped.append(keep.tile([P, T, 4], BF16, align_bytes=ALIGN, name="grouped_%d" % a))
            codes.append(keep.tile([P, T], U32, align_bytes=ALIGN, name="codes_%d" % a))
            scales.append(keep.tile([P, T], U8, align_bytes=ALIGN, name="scales_%d" % a))

        def interleave(engine_copy, a, lo, hi):
            base, piece = [(begin, tile) for begin, end, tile in raw[a] if begin <= lo and hi <= end][0]
            engine_copy(
                out=grouped[a][:, lo:hi, :].rearrange("p (c i) j -> p c j i", i=4),
                in_=piece[:, :, lo - base : hi - base].rearrange("p j (c i) -> p c j i", i=4),
            )

        def copy_v(a, lo, hi):
            interleave(nc.vector.tensor_copy, a, lo, hi)

        def copy_s(a, lo, hi):
            interleave(nc.scalar.copy, a, lo, hi)

        def quantize(a, lo, hi):
            nc.vector.quantize_mx(
                out=codes[a][:, lo:hi].bitcast(FP8X4),
                scales=scales[a][:, lo:hi],
                in_=grouped[a][:, lo:hi, :].rearrange("p w j -> p (w j)"),
            )

        banks = {}
        filled = {}

        def sums(kind, m, lo, hi):
            key, tag, at = place(kind, m, lo)
            return banks[key][:, at : at + hi - lo]

        def multiply(kind, a, m, lo, hi):
            key, tag, at = place(kind, m, lo)
            if key not in banks:
                banks[key] = psum.tile([P, BANK], F32, name=key, tag=tag)
            before = filled.get(key, 0)
            filled[key] = before + hi - lo
            if kind == "g":
                words = w4[a][:, 2 * P * m : 2 * P * (m + 1)].bitcast(FP4X4)
                word_scales = sc4[:, M * a + P * m : M * a + P * (m + 1)]
            else:
                words = w8[a][:, 4 * P * m : 4 * P * (m + 1)].bitcast(FP8X4)
                word_scales = sc8[4 * a : P, P * m : P * (m + 1)]
            nc.tensor.matmul_mx(
                out=sums(kind, m, lo, hi),
                lhsT=words,
                lhsT_scale=word_scales,
                rhs=codes[a][:, lo:hi].bitcast(FP8X4),
                rhs_scale=scales[a][:, lo:hi],
                start=(before == 0),
                stop=(filled[key] == PASSES * BANK),
            )

        gate = keep.tile([P, ROW_TILES * T], F32, align_bytes=ALIGN, name="gate")
        res = {}

        def result_tile(rows, lo, hi):
            tile = keep.tile([P, len(rows), hi - lo], F32, align_bytes=ALIGN, name="res_%d_%d" % (rows[0], lo))
            for i, m in enumerate(rows):
                res.setdefault(m, []).append((lo, hi, tile[:, i, :]))
            return rows, lo, hi, tile

        def silu(m, lo, hi):
            nc.scalar.activation(out=gate[:, T * m + lo : T * m + hi], in_=sums("g", m, lo, hi), func=ACT.Silu)

        def product(m, lo, hi):
            base, row = [(begin, tile) for begin, end, tile in res[m] if begin <= lo and hi <= end][0]
            nc.vector.tensor_tensor(
                out=row[:, lo - base : hi - base],
                in0=sums("u", m, lo, hi),
                in1=gate[:, T * m + lo : T * m + hi],
                op=ALU.mult,
            )

        def store(rows, lo, hi, tile):
            nc.sync.dma_start(
                out=out[P * rows[0] : P * (rows[-1] + 1), lo:hi].rearrange("(m p) w -> p m w", p=P), in_=tile[:]
            )

        warm = keep.tile([P, 1], F32, name="warm")
        nc.scalar.activation(out=warm[:], in_=sc8[:, M : M + 4].bitcast(F32), func=ACT.Silu)

        rows = list(range(ROW_TILES))
        left, right = HALF, HALF + STRIP
        first_store = result_tile(rows, 0, HALF)
        left_stores = [result_tile(pair, left, right) for pair in (rows[:2], rows[2:])]
        last_stores = [result_tile([m], right, T) for m in rows]

        load_sc8()
        load_x(0, 0, HALF)
        load_sc4()
        load_w4(0, PASSES)
        load_w8(0, 1)
        load_x(1, 0, HALF)
        load_w8(1, 1)
        load_x(2, 0, HALF)
        load_x(3, 0, HALF)
        load_w8(2, 1)
        load_x(0, left, right)
        load_w8(3, 1)
        for a in range(1, PASSES):
            load_x(a, left, right)
        for a in range(PASSES):
            load_x(a, right, T)

        def copies(a, lo, share):
            if share > 0:
                copy_v(a, lo, lo + share)
            if share < STRIP:
                copy_s(a, lo + share, lo + STRIP)

        def prepare(a, base, shares):
            for lo, share in zip((base, base + STRIP), shares):
                copies(a, lo, share)
            for lo in (base, base + STRIP):
                quantize(a, lo, lo + STRIP)

        def whole(kind, a, tiles):
            for m in tiles:
                multiply(kind, a, m, 0, HALF)

        def strip(a, lo, tiles, kinds="gu"):
            for m in tiles:
                for kind in kinds:
                    multiply(kind, a, m, lo, lo + STRIP)

        for a in range(LAST):
            prepare(a, 0, (160, 160))
            whole("g", a, rows)
            if a < 2:
                whole("u", a, rows)
        prepare(LAST, 0, (160, 160))
        whole("u", 2, rows[:3])
        for lo in (0, STRIP):
            for m in rows[:3]:
                multiply("g", LAST, m, lo, lo + STRIP)
        whole("g", LAST, rows[3:])
        whole("u", 2, rows[3:])
        whole("u", LAST, rows)
        copies(0, left, 160)
        quantize(0, left, right)
        for m in rows:
            silu(m, 0, HALF)
        strip(0, left, rows)
        for at in (left, left + P):
            copy_v(1, at, at + P)
        for at in (left, left + P):
            quantize(1, at, at + P)
        product(0, 0, HALF)
        strip(1, left, rows)
        for a in (2, 3):
            copies(a, left, 96)
            product(a - 1, 0, HALF)
            quantize(a, left, right)
            strip(a, left, rows)
        copies(0, right, 96)
        product(3, 0, HALF)
        quantize(0, right, T)
        strip(0, right, [0, 1])
        strip(0, right, [2, 3], "g")
        strip(0, right, [2, 3], "u")
        for a in (1, 2):
            copies(a, right, 160)
            if a == 2:
                product(0, left, right)
            quantize(a, right, T)
            strip(a, right, [0, 1])
            strip(a, right, [2, 3], "g")
            for m in (2 * a - 2, 2 * a - 1):
                silu(m, left, right)
        strip(1, right, [2, 3], "u")
        copy_v(LAST, right, right + P)
        copy_v(LAST, right + P, right + 160)
        copy_s(LAST, right + 160, T)
        quantize(LAST, right, right + P)
        quantize(LAST, right + P, T)
        for m in rows[1:]:
            product(m, left, right)
        store(*first_store)
        for tile in left_stores:
            store(*tile)
        strip(LAST, right, [0, 1])
        strip(LAST, right, [2, 3], "g")
        for a in (2, 3):
            strip(a, right, [2, 3], "u")
        for m in rows:
            silu(m, right, T)
            product(m, right, T)
            store(*last_stores[m])
